import numpy as np
import ml_dtypes


def mxq(x, axis, fmt="e4m3"):
    dtype, down = {"e4m3": (ml_dtypes.float8_e4m3fn, 7), "e5m2": (ml_dtypes.float8_e5m2, 14)}[fmt]
    v = np.moveaxis(np.asarray(x, np.float32).astype(ml_dtypes.bfloat16).astype(np.float64), axis, -1)
    blocks = v.reshape(v.shape[:-1] + (-1, 32))
    amax = np.abs(blocks).max(-1, keepdims=True)
    byte = np.maximum(np.where(amax > 0, np.frexp(amax)[1] - 1 + 127, 0) - down, 1)
    scale = np.exp2(byte - 127.0)
    codes = (blocks / scale).astype(np.float32).astype(dtype).astype(np.float64)
    return np.moveaxis((codes * scale).reshape(v.shape), -1, axis)


WIDE = False


def mx_kscale(k):
    if not WIDE:
        return np.ones(k)
    levels = np.array([10, -10, 5, -5, 0])
    if k % 512:
        return np.exp2(np.random.permutation(np.resize(levels, k // 32))).repeat(32)
    a = np.empty((k // 512, 16))
    for p in range(k // 512):
        a[p, :8] = np.random.permutation(np.resize(levels, 8))
        for g in range(8):
            far = levels[np.abs(levels - a[p, g]) >= 10]
            a[p, g + 8] = far[np.random.randint(len(far))]
    return np.exp2(a.ravel()).repeat(32)


def f64(x):
    return np.asarray(x).astype(np.float64)


def striped(idx):
    return np.tile(idx.reshape(-1, 16).T, (8, 1)).astype(np.uint16)


def unstriped(offs):
    return offs[:16].T.reshape(-1).astype(np.int64)


def pack_weight(w):
    k, n = w.shape
    w = f64(np.asarray(w, np.float32).astype(ml_dtypes.bfloat16)).reshape(k // 32, 32, n)
    amax = np.abs(w).max(1)
    byte = np.clip(np.where(amax > 0, np.frexp(amax)[1] - 1 + 127 - 7, 1), 1, 254)
    scaled = (w * np.exp2(127.0 - byte)[:, None, :]).reshape(k, n).astype(np.float32)
    words = np.ascontiguousarray(scaled.reshape(k // 512, 128, 4, n).transpose(0, 1, 3, 2)).astype(ml_dtypes.float8_e4m3fn).view(np.uint8)
    return words, np.ascontiguousarray(byte.astype(np.uint8).reshape(k // 512, 16, n))


def unpack_weight(words, scales):
    g, p, n, _ = words.shape
    vals = np.ascontiguousarray(words).view(ml_dtypes.float8_e4m3fn).astype(np.float64) * np.repeat(np.exp2(scales.astype(np.float64) - 127.0), 8, axis=1)[..., None]
    return vals.transpose(0, 1, 3, 2).reshape(g * 512, n)


E2M1 = np.array([0.0, 0.5, 1.0, 1.5, 2.0, 3.0, 4.0, 6.0, -0.0, -0.5, -1.0, -1.5, -2.0, -3.0, -4.0, -6.0])


def pack_fp4(w):
    k, n = w.shape
    w = f64(np.asarray(w, np.float32).astype(ml_dtypes.bfloat16)).reshape(k // 32, 32, n)
    amax = np.abs(w).max(1)
    mant, ex = np.frexp(amax / 6.0)
    byte = np.clip(np.where(amax > 0, np.where(mant > 0.5, ex, ex - 1) + 127, 1), 1, 254)
    scaled = (w * np.exp2(127.0 - byte)[:, None, :]).reshape(k, n).astype(np.float32)
    c = np.ascontiguousarray(scaled.reshape(k // 512, 128, 4, n).transpose(0, 1, 3, 2)).astype(ml_dtypes.float4_e2m1fn).view(np.uint8) & 0xF
    words = (c[..., 0::2] | (c[..., 1::2] << 4)).reshape(k // 512, 128, 2 * n)
    return np.ascontiguousarray(words), np.ascontiguousarray(byte.astype(np.uint8).reshape(k // 512, 16, n))


def unpack_fp4(words, scales):
    g, _, n = scales.shape
    words = np.ascontiguousarray(words).reshape(g, 128, n, 2)
    nib = np.empty((g, 128, n, 4), np.uint8)
    nib[..., 0::2] = words & 0xF
    nib[..., 1::2] = words >> 4
    vals = E2M1[nib] * np.repeat(np.exp2(scales.astype(np.float64) - 127.0), 8, axis=1)[..., None]
    return vals.transpose(0, 1, 3, 2).reshape(g * 512, n)


def planes(y):
    n, m = y.shape
    v = y.astype(np.float32).astype(ml_dtypes.bfloat16).astype(np.float64).reshape(n // 32, 32, m)
    top = np.abs(v).max(1)
    byte = np.clip(np.where(top > 0, np.frexp(top)[1] - 1 + 127 - 7, 1), 1, 254)
    codes = (v * np.exp2(127.0 - byte)[:, None, :]).reshape(n, m).astype(np.float32).astype(ml_dtypes.float8_e4m3fn).view(np.uint8)
    words = codes.reshape(n // 512, 128, 4, m).transpose(0, 1, 3, 2)
    return np.ascontiguousarray(words), np.ascontiguousarray(byte.astype(np.uint8).reshape(n // 512, 16, m))


def sigmoid(v):
    return 1.0 / (1.0 + np.exp(-np.maximum(v, -700.0)))


K, T, S, W, H = 1024, 1024, 512, 1024, 512


def setup_inputs():
    n = np.random.standard_normal
    s = mx_kscale(K)[:, None]
    u = mx_kscale(H)
    packed_xT = pack_weight(n((K, T)) * s)
    packed_eT = pack_weight(n((K, W)) * s)
    packed_w3 = pack_fp4(n((H, H)) / np.sqrt(H) / u[:, None])
    return {
        "x_words": packed_xT[0],
        "x_scales": packed_xT[1],
        "e_words": packed_eT[0],
        "e_scales": packed_eT[1],
        "w1": (n((K, H)) / np.sqrt(2 * K) / s * u).astype(np.float32),
        "w2": (n((K, H)) / np.sqrt(2 * K) / s * u).astype(np.float32),
        "w3_words": packed_w3[0],
        "w3_scales": packed_w3[1],
        "skip": (n((H, S)) * u[:, None]).astype(np.float32),
        "offs": striped(np.random.permutation(T)[:S]),
        "tok": striped(np.random.permutation(W)[:S]),
    }


def reference(x_words, x_scales, e_words, e_scales, w1, w2, w3_words, w3_scales, skip, offs, tok):
    xq = unpack_weight(x_words, x_scales)[:, unstriped(offs)]
    e_tok = unpack_weight(e_words, e_scales)[:, unstriped(tok)]
    h = mxq(f64(w1), 0, "e4m3").T @ xq + mxq(f64(w2), 0, "e4m3").T @ e_tok
    g = sigmoid(unpack_fp4(w3_words, w3_scales).T @ mxq(h, 0, "e4m3"))
    out_0 = f64(skip) + g * (h - f64(skip))
    return (out_0,) + planes(out_0)

@@ -1,0 +1,204 @@
+from contextlib import ExitStack
+
+import concourse.mybir as mybir
+
+K, T, S, H = 1024, 1024, 512, 512
+FLOPS = 2 * (2 * K * H * S) + 2 * H * H * S
+
+F32 = mybir.dt.float32
+BF16 = mybir.dt.bfloat16
+I32 = mybir.dt.int32
+U32 = mybir.dt.uint32
+U16 = mybir.dt.uint16
+U8 = mybir.dt.uint8
+FP8X4 = mybir.dt.float8_e4m3fn_x4
+FP4X4 = mybir.dt.float4_e2m1fn_x4
+SIGMOID = mybir.ActivationFunctionType.Sigmoid
+SUB = mybir.AluOpType.subtract
+MULT = mybir.AluOpType.mult
+ADD = mybir.AluOpType.add
+
+P = 128
+PACK = 4
+KP = P * PACK
+CH = 128
+NCH = S // CH
+LC = CH // 16
+V_SHARE_M = 88
+
+
+def tile_picked_zhwy_lin_po_kernel(
+    tc, x_words, x_scales, e_words, e_scales, w1, w2, w3_words, w3_scales, skip, offs, tok, out_0, out_1, out_2
+):
+    nc = tc.nc
+    with ExitStack() as ctx:
+        keep = ctx.enter_context(tc.tile_pool(name="keep", bufs=1))
+        psum = ctx.enter_context(tc.psum_pool(name="psum", bufs=1))
+
+        def sb(name, shape, dtype):
+            return keep.tile(shape, dtype, name=name, align_bytes=64)
+
+        offs_sb = keep.tile([P, S // 16], U16, name="offs_sb")
+        tok_sb = keep.tile([P, S // 16], U16, name="tok_sb")
+
+        xs_win = sb("xs_win", [P, T], U8)
+        es_win = sb("es_win", [P, T], U8)
+        w3s_raw = sb("w3s_raw", [P, H], U8)
+        nc.gpsimd.memset(xs_win[:].bitcast(I32), 0)
+        nc.vector.memset(es_win[:].bitcast(I32), 0)
+        nc.vector.memset(w3s_raw[:].bitcast(I32), 0)
+
+        w_src = [w1[0:KP, :], w1[KP:K, :], w2[0:KP, :], w2[KP:K, :]]
+        t_src = [x_words[0], x_words[1], e_words[0], e_words[1]]
+        w_raw = [keep.tile([P, PACK, H], F32, name=f"w_raw{g}", tag=f"raw{g}", align_bytes=64) for g in range(4)]
+        win = [sb(f"win{g}", [P, T], U32) for g in range(4)]
+
+        def load_w(g):
+            nc.sync.dma_start(out=w_raw[g][:], in_=w_src[g].rearrange("(p j) c -> p j c", j=PACK))
+
+        def load_t(g):
+            nc.sync.dma_start(out=win[g][:].bitcast(I32), in_=t_src[g].rearrange("p n t -> p (n t)").bitcast(I32))
+
+        w3_raw = sb("w3_raw", [P, 2 * H], U8)
+
+        load_w(0)
+        nc.sync.dma_start(offs_sb[:], offs)
+        nc.sync.dma_start(out=w3_raw[:].bitcast(I32), in_=w3_words[0].bitcast(I32))
+        for q in range(4):
+            nc.gpsimd.dma_start(out=xs_win[32 * q : 32 * q + 8, :].bitcast(I32), in_=x_scales[:, 4 * q : 4 * q + 4, :].bitcast(I32))
+        for q in range(4):
+            nc.gpsimd.dma_start(out=es_win[32 * q : 32 * q + 8, :].bitcast(I32), in_=e_scales[:, 4 * q : 4 * q + 4, :].bitcast(I32))
+        load_t(0)
+        nc.sync.dma_start(tok_sb[:], tok)
+        for q in range(4):
+            nc.sync.dma_start(out=w3s_raw[32 * q : 32 * q + 4, :].bitcast(I32), in_=w3_scales[0, 4 * q : 4 * q + 4, :].bitcast(I32))
+        load_w(1)
+        load_t(1)
+        load_w(2)
+        load_w(3)
+        load_t(2)
+        load_t(3)
+
+        w_bf = [sb(f"w_bf{g}", [P, PACK * H], BF16) for g in range(4)]
+        w_codes = [sb(f"w_codes{g}", [P, H], U32) for g in range(4)]
+        w_sc = [sb(f"w_sc{g}", [P, H], U8) for g in range(4)]
+        picked = [sb(f"picked{g}", [P, S], U32) for g in range(4)]
+        xs_picked = sb("xs_picked", [P, S], U8)
+        es_picked = sb("es_picked", [P, S], U8)
+        w3_dealt = sb("w3_dealt", [P, 2 * H], U8)
+        w3s_dealt = sb("w3s_dealt", [P, H], U8)
+
+        def cast_views(g):
+            dst = w_bf[g][:].rearrange("p (t m j) -> p m j t", t=PACK, j=PACK)
+            src = w_raw[g][:].rearrange("p j (m t) -> p m j t", t=PACK)
+            return dst, src
+
+        def quant_w(g):
+            nc.vector.quantize_mx(out=w_codes[g][:].bitcast(FP8X4), scales=w_sc[g][:], in_=w_bf[g][:])
+
+        def gather(g, c0, c1):
+            lst = offs_sb if g < 2 else tok_sb
+            nc.vector.tensor_copy(picked[g][:, CH * c0 : CH * c1], win[g][:].indirect(lst[:, LC * c0 : LC * c1]))
+
+        h_ps = [psum.tile([P, PACK, CH], F32, name=f"h_ps{c}") for c in range(NCH)]
+        u_ps = [psum.tile([P, PACK, CH], F32, name=f"u_ps{c}") for c in range(NCH)]
+
+        def h_pass(c, t, g):
+            cols = slice(CH * c, CH * (c + 1))
+            mc = slice(P * t, P * (t + 1))
+            planes = xs_picked if g < 2 else es_picked
+            nc.tensor.matmul_mx(
+                out=h_ps[c][:, t, :],
+                lhsT=w_codes[g][:, mc].bitcast(FP8X4),
+                lhsT_scale=w_sc[g][:, mc],
+                rhs=picked[g][:, cols].bitcast(FP8X4),
+                rhs_scale=planes[4 * (g % 2) : P, cols],
+                start=(g == 0),
+                stop=(g == 3),
+            )
+
+        nc.vector.tensor_copy(xs_picked[:], xs_win[:].indirect(offs_sb[:]))
+        dst, src = cast_views(0)
+        nc.scalar.copy(dst, src)
+        gather(0, 0, NCH)
+        quant_w(0)
+        nc.vector.tensor_copy(
+            w3_dealt[:].rearrange("p (t m b) -> p m t b", t=PACK, b=2), w3_raw[:].rearrange("p (m t b) -> p m t b", t=PACK, b=2)
+        )
+        nc.vector.tensor_copy(w3s_dealt[:].rearrange("p (t m) -> p m t", t=PACK), w3s_raw[:].rearrange("p (m t) -> p m t", t=PACK))
+        nc.vector.tensor_copy(es_picked[:], es_win[:].indirect(tok_sb[:]))
+        dst, src = cast_views(1)
+        nc.scalar.copy(dst, src)
+        gather(1, 0, NCH)
+        quant_w(1)
+        dst, src = cast_views(2)
+        nc.scalar.copy(dst, src)
+        quant_w(2)
+        dst, src = cast_views(3)
+        nc.vector.tensor_copy(dst[:, :V_SHARE_M], src[:, :V_SHARE_M])
+        nc.scalar.copy(dst[:, V_SHARE_M:], src[:, V_SHARE_M:])
+        quant_w(3)
+        skip_sb = [keep.tile([P, PACK, 2 * CH], F32, name=f"skip{a}", tag=f"raw{a + 1}", align_bytes=64) for a in range(2)]
+        skip_v = skip.rearrange("(p t) j -> p t j", t=PACK)
+        for a in range(2):
+            nc.sync.dma_start(out=skip_sb[a][:], in_=skip_v[:, :, 2 * CH * a : 2 * CH * (a + 1)])
+
+        h_bf = [sb(f"h_bf{c}", [P, CH * PACK], BF16) for c in range(NCH)]
+        h_codes = [sb(f"h_codes{c}", [P, CH], U32) for c in range(NCH)]
+        h_sc = [sb(f"h_sc{c}", [P, CH], U8) for c in range(NCH)]
+        gate = [sb(f"gate{c}", [P, PACK, CH], F32) for c in range(NCH)]
+        diff = [sb(f"diff{c}", [P, PACK, CH], F32) for c in range(NCH)]
+        prod = [sb(f"prod{c}", [P, PACK, CH], F32) for c in range(NCH)]
+        res = [sb(f"res{c}", [P, PACK, CH], F32) for c in range(NCH)]
+        res_bf = [sb(f"res_bf{c}", [P, CH * PACK], BF16) for c in range(NCH)]
+        res_codes = [sb(f"res_codes{c}", [P, CH], U32) for c in range(NCH)]
+        res_sc = sb("res_sc", [P, S], U8)
+        out_v = out_0.rearrange("(p t) j -> p t j", t=PACK)
+        words_v = out_1[0].rearrange("p n t -> p (n t)").bitcast(I32)
+
+        def skip_of(c):
+            return skip_sb[c // 2][:, :, CH * (c % 2) : CH * (c % 2 + 1)]
+
+        def stage_gate(c):
+            gather(2, c, c + 1)
+            gather(3, c, c + 1)
+            for t in range(PACK):
+                for g in range(4):
+                    h_pass(c, t, g)
+            nc.scalar.copy(h_bf[c][:].rearrange("p (n t) -> p n t", t=PACK), h_ps[c][:].rearrange("p t n -> p n t"))
+            nc.vector.quantize_mx(out=h_codes[c][:].bitcast(FP8X4), scales=h_sc[c][:], in_=h_bf[c][:])
+            for t in range(PACK):
+                nc.tensor.matmul_mx(
+                    out=u_ps[c][:, t, :],
+                    lhsT=w3_dealt[:, 2 * P * t : 2 * P * (t + 1)].bitcast(FP4X4),
+                    lhsT_scale=w3s_dealt[:, P * t : P * (t + 1)],
+                    rhs=h_codes[c][:].bitcast(FP8X4),
+                    rhs_scale=h_sc[c][:],
+                    start=True,
+                    stop=True,
+                )
+            nc.scalar.activation(gate[c][:], u_ps[c][:], SIGMOID)
+
+        def stage_mix(c):
+            nc.vector.tensor_tensor(diff[c][:], h_ps[c][:], skip_of(c), SUB)
+            nc.vector.tensor_tensor(prod[c][:], gate[c][:], diff[c][:], MULT)
+            nc.vector.tensor_tensor(res[c][:], prod[c][:], skip_of(c), ADD)
+            nc.sync.dma_start(out=out_v[:, :, CH * c : CH * (c + 1)], in_=res[c][:])
+
+        def stage_planes(c):
+            nc.scalar.copy(
+                res_bf[c][:].rearrange("p (n i t) -> p n t i", i=4, t=PACK), res[c][:].rearrange("p t (n i) -> p n t i", i=4)
+            )
+            nc.vector.quantize_mx(out=res_codes[c][:].bitcast(FP8X4), scales=res_sc[:, CH * c : CH * (c + 1)], in_=res_bf[c][:])
+            nc.sync.dma_start(out=words_v[:, CH * c : CH * (c + 1)], in_=res_codes[c][:].bitcast(I32))
+
+        for step in range(NCH + 2):
+            if step < NCH:
+                stage_gate(step)
+            if 1 <= step <= NCH:
+                stage_mix(step - 1)
+            if step >= 2:
+                stage_planes(step - 2)
+        for q in range(4):
+            eng = nc.sync if q % 2 == 0 else nc.scalar
+            eng.dma_start(out=out_2[0, 4 * q : 4 * q + 4, :].bitcast(I32), in_=res_sc[32 * q : 32 * q + 4, :].bitcast(I32))

@@ -24,7 +24,7 @@ KP = P * PACK
 CH = 128
 NCH = S // CH
 LC = CH // 16
-V_SHARE_M = 88
+V_SHARE_M = 40
 
 
 def tile_picked_zhwy_lin_po_kernel(
@@ -42,47 +42,60 @@ def tile_picked_zhwy_lin_po_kernel(
         tok_sb = keep.tile([P, S // 16], U16, name="tok_sb")
 
         xs_win = sb("xs_win", [P, T], U8)
-        es_win = sb("es_win", [P, T], U8)
-        w3s_raw = sb("w3s_raw", [P, H], U8)
-        nc.gpsimd.memset(xs_win[:].bitcast(I32), 0)
+        es_win = keep.tile([P, T], U8, name="es_win", tag="es_slot", align_bytes=64)
+        w3s_raw = keep.tile([P, H], U8, name="w3s_raw", tag="w3s_slot", align_bytes=64)
+        table_in = sb("table_in", [P, 1], F32)
+        table_out = sb("table_out", [P, 1], F32)
+        nc.vector.memset(table_in[:], 0.0)
+        nc.scalar.activation(table_out[:], table_in[:], SIGMOID)
+        nc.vector.memset(xs_win[:].bitcast(I32), 0)
         nc.vector.memset(es_win[:].bitcast(I32), 0)
         nc.vector.memset(w3s_raw[:].bitcast(I32), 0)
 
         w_src = [w1[0:KP, :], w1[KP:K, :], w2[0:KP, :], w2[KP:K, :]]
-        t_src = [x_words[0], x_words[1], e_words[0], e_words[1]]
-        w_raw = [keep.tile([P, PACK, H], F32, name=f"w_raw{g}", tag=f"raw{g}", align_bytes=64) for g in range(4)]
-        win = [sb(f"win{g}", [P, T], U32) for g in range(4)]
+        w_raw = [sb(f"w_raw{g}", [P, PACK, H], F32) for g in range(4)]
+        x_win = [sb(f"x_win{g}", [P, T], U32) for g in range(2)]
+        e_win = sb("e_win", [P, 2, T], U32)
 
         def load_w(g):
             nc.sync.dma_start(out=w_raw[g][:], in_=w_src[g].rearrange("(p j) c -> p j c", j=PACK))
 
-        def load_t(g):
-            nc.sync.dma_start(out=win[g][:].bitcast(I32), in_=t_src[g].rearrange("p n t -> p (n t)").bitcast(I32))
+        def load_x(g):
+            nc.sync.dma_start(out=x_win[g][:].bitcast(I32), in_=x_words[g].rearrange("p n t -> p (n t)").bitcast(I32))
 
         w3_raw = sb("w3_raw", [P, 2 * H], U8)
 
+        def load_planes(dst, src):
+            for q in range(4):
+                nc.sync.dma_start(out=dst[32 * q : 32 * q + 8, :].bitcast(I32), in_=src[:, 4 * q : 4 * q + 4, :].bitcast(I32))
+
+        skip_sb = [sb(f"skip{a}", [P, PACK, 2 * CH], F32) for a in range(2)]
+        skip_v = skip.rearrange("(p t) j -> p t j", t=PACK)
         load_w(0)
         nc.sync.dma_start(offs_sb[:], offs)
         nc.sync.dma_start(out=w3_raw[:].bitcast(I32), in_=w3_words[0].bitcast(I32))
-        for q in range(4):
-            nc.gpsimd.dma_start(out=xs_win[32 * q : 32 * q + 8, :].bitcast(I32), in_=x_scales[:, 4 * q : 4 * q + 4, :].bitcast(I32))
-        for q in range(4):
-            nc.gpsimd.dma_start(out=es_win[32 * q : 32 * q + 8, :].bitcast(I32), in_=e_scales[:, 4 * q : 4 * q + 4, :].bitcast(I32))
-        load_t(0)
-        nc.sync.dma_start(tok_sb[:], tok)
+        load_planes(xs_win, x_scales)
+        load_w(1)
         for q in range(4):
             nc.sync.dma_start(out=w3s_raw[32 * q : 32 * q + 4, :].bitcast(I32), in_=w3_scales[0, 4 * q : 4 * q + 4, :].bitcast(I32))
-        load_w(1)
-        load_t(1)
         load_w(2)
+        load_x(0)
+        nc.sync.dma_start(tok_sb[:], tok)
+        load_planes(es_win, e_scales)
         load_w(3)
-        load_t(2)
-        load_t(3)
+        load_x(1)
+        nc.sync.dma_start(out=e_win[:].bitcast(I32), in_=e_words.rearrange("o p n t -> p o (n t)").bitcast(I32))
+        for a in range(2):
+            nc.sync.dma_start(out=skip_sb[a][:], in_=skip_v[:, :, 2 * CH * a : 2 * CH * (a + 1)])
 
         w_bf = [sb(f"w_bf{g}", [P, PACK * H], BF16) for g in range(4)]
         w_codes = [sb(f"w_codes{g}", [P, H], U32) for g in range(4)]
-        w_sc = [sb(f"w_sc{g}", [P, H], U8) for g in range(4)]
-        picked = [sb(f"picked{g}", [P, S], U32) for g in range(4)]
+        sc_tags = ["w_sc0", "w3s_slot", "es_slot", "w_sc3"]
+        w_sc = []
+        x_picked = [sb(f"x_picked{g}", [P, S], U32) for g in range(2)]
+        e_spans = [(0, 1), (1, 2), (2, 4)]
+        e_tiles = [[sb(f"e_picked{g}_{a}", [P, CH * (b - a)], U32) for a, b in e_spans] for g in range(2)]
+        e_picked = [[t[0][:], t[1][:], t[2][:, 0:CH], t[2][:, CH : 2 * CH]] for t in e_tiles]
         xs_picked = sb("xs_picked", [P, S], U8)
         es_picked = sb("es_picked", [P, S], U8)
         w3_dealt = sb("w3_dealt", [P, 2 * H], U8)
@@ -94,11 +107,15 @@ def tile_picked_zhwy_lin_po_kernel(
             return dst, src
 
         def quant_w(g):
+            w_sc.append(keep.tile([P, H], U8, name=f"w_sc{g}", tag=sc_tags[g], align_bytes=64))
             nc.vector.quantize_mx(out=w_codes[g][:].bitcast(FP8X4), scales=w_sc[g][:], in_=w_bf[g][:])
 
-        def gather(g, c0, c1):
-            lst = offs_sb if g < 2 else tok_sb
-            nc.vector.tensor_copy(picked[g][:, CH * c0 : CH * c1], win[g][:].indirect(lst[:, LC * c0 : LC * c1]))
+        def gather_x(g):
+            nc.vector.tensor_copy(x_picked[g][:], x_win[g][:].indirect(offs_sb[:]))
+
+        def gather_e(g, c):
+            a, b = e_spans[c]
+            nc.vector.tensor_copy(e_tiles[g][c][:], e_win[:, g, :].indirect(tok_sb[:, LC * a : LC * b]))
 
         h_ps = [psum.tile([P, PACK, CH], F32, name=f"h_ps{c}") for c in range(NCH)]
         u_ps = [psum.tile([P, PACK, CH], F32, name=f"u_ps{c}") for c in range(NCH)]
@@ -111,37 +128,48 @@ def tile_picked_zhwy_lin_po_kernel(
                 out=h_ps[c][:, t, :],
                 lhsT=w_codes[g][:, mc].bitcast(FP8X4),
                 lhsT_scale=w_sc[g][:, mc],
-                rhs=picked[g][:, cols].bitcast(FP8X4),
+                rhs=(x_picked[g][:, cols] if g < 2 else e_picked[g - 2][c]).bitcast(FP8X4),
                 rhs_scale=planes[4 * (g % 2) : P, cols],
                 start=(g == 0),
                 stop=(g == 3),
             )
 
+        def warm_up(g, codes, planes):
+            nc.tensor.matmul_mx(
+                out=u_ps[NCH - 1][:].rearrange("p t n -> p (t n)"),
+                lhsT=w_codes[g][:, 0:P].bitcast(FP8X4),
+                lhsT_scale=w_sc[g][:, 0:P],
+                rhs=codes[:].bitcast(FP8X4),
+                rhs_scale=planes[:],
+                start=True,
+                stop=True,
+            )
+
         nc.vector.tensor_copy(xs_picked[:], xs_win[:].indirect(offs_sb[:]))
+        nc.vector.tensor_copy(
+            w3_dealt[:].rearrange("p (t m b) -> p t m b", t=PACK, b=2), w3_raw[:].rearrange("p (m t b) -> p t m b", t=PACK, b=2)
+        )
         dst, src = cast_views(0)
         nc.scalar.copy(dst, src)
-        gather(0, 0, NCH)
         quant_w(0)
-        nc.vector.tensor_copy(
-            w3_dealt[:].rearrange("p (t m b) -> p m t b", t=PACK, b=2), w3_raw[:].rearrange("p (m t b) -> p m t b", t=PACK, b=2)
-        )
-        nc.vector.tensor_copy(w3s_dealt[:].rearrange("p (t m) -> p m t", t=PACK), w3s_raw[:].rearrange("p (m t) -> p m t", t=PACK))
-        nc.vector.tensor_copy(es_picked[:], es_win[:].indirect(tok_sb[:]))
         dst, src = cast_views(1)
         nc.scalar.copy(dst, src)
-        gather(1, 0, NCH)
+        nc.vector.tensor_copy(w3s_dealt[:].rearrange("p (t m) -> p t m", t=PACK), w3s_raw[:].rearrange("p (m t) -> p t m", t=PACK))
         quant_w(1)
         dst, src = cast_views(2)
         nc.scalar.copy(dst, src)
+        gather_x(0)
+        nc.vector.tensor_copy(es_picked[:], es_win[:].indirect(tok_sb[:]))
         quant_w(2)
         dst, src = cast_views(3)
         nc.vector.tensor_copy(dst[:, :V_SHARE_M], src[:, :V_SHARE_M])
         nc.scalar.copy(dst[:, V_SHARE_M:], src[:, V_SHARE_M:])
+        gather_x(1)
         quant_w(3)
-        skip_sb = [keep.tile([P, PACK, 2 * CH], F32, name=f"skip{a}", tag=f"raw{a + 1}", align_bytes=64) for a in range(2)]
-        skip_v = skip.rearrange("(p t) j -> p t j", t=PACK)
-        for a in range(2):
-            nc.sync.dma_start(out=skip_sb[a][:], in_=skip_v[:, :, 2 * CH * a : 2 * CH * (a + 1)])
+        for rep in range(3):
+            warm_up(2, x_picked[0], xs_picked)
+        for rep in range(2):
+            warm_up(0, x_picked[1], xs_picked)
 
         h_bf = [sb(f"h_bf{c}", [P, CH * PACK], BF16) for c in range(NCH)]
         h_codes = [sb(f"h_codes{c}", [P, CH], U32) for c in range(NCH)]
@@ -149,9 +177,11 @@ def tile_picked_zhwy_lin_po_kernel(
         gate = [sb(f"gate{c}", [P, PACK, CH], F32) for c in range(NCH)]
         diff = [sb(f"diff{c}", [P, PACK, CH], F32) for c in range(NCH)]
         prod = [sb(f"prod{c}", [P, PACK, CH], F32) for c in range(NCH)]
-        res = [sb(f"res{c}", [P, PACK, CH], F32) for c in range(NCH)]
-        res_bf = [sb(f"res_bf{c}", [P, CH * PACK], BF16) for c in range(NCH)]
-        res_codes = [sb(f"res_codes{c}", [P, CH], U32) for c in range(NCH)]
+        spans = [(0, 2), (2, 3), (3, 4)]
+        res_t = [sb(f"res{i}", [P, PACK, CH * (b - a)], F32) for i, (a, b) in enumerate(spans)]
+        res = [res_t[0][:, :, 0:CH], res_t[0][:, :, CH : 2 * CH], res_t[1][:], res_t[2][:]]
+        res_bf = [sb(f"res_bf{i}", [P, CH * PACK * (b - a)], BF16) for i, (a, b) in enumerate(spans)]
+        res_codes = [sb(f"res_codes{i}", [P, CH * (b - a)], U32) for i, (a, b) in enumerate(spans)]
         res_sc = sb("res_sc", [P, S], U8)
         out_v = out_0.rearrange("(p t) j -> p t j", t=PACK)
         words_v = out_1[0].rearrange("p n t -> p (n t)").bitcast(I32)
@@ -160,8 +190,9 @@ def tile_picked_zhwy_lin_po_kernel(
             return skip_sb[c // 2][:, :, CH * (c % 2) : CH * (c % 2 + 1)]
 
         def stage_gate(c):
-            gather(2, c, c + 1)
-            gather(3, c, c + 1)
+            if c < len(e_spans):
+                gather_e(0, c)
+                gather_e(1, c)
             for t in range(PACK):
                 for g in range(4):
                     h_pass(c, t, g)
@@ -179,26 +210,42 @@ def tile_picked_zhwy_lin_po_kernel(
                 )
             nc.scalar.activation(gate[c][:], u_ps[c][:], SIGMOID)
 
-        def stage_mix(c):
+        def stage_diff(c):
             nc.vector.tensor_tensor(diff[c][:], h_ps[c][:], skip_of(c), SUB)
-            nc.vector.tensor_tensor(prod[c][:], gate[c][:], diff[c][:], MULT)
-            nc.vector.tensor_tensor(res[c][:], prod[c][:], skip_of(c), ADD)
-            nc.sync.dma_start(out=out_v[:, :, CH * c : CH * (c + 1)], in_=res[c][:])
 
-        def stage_planes(c):
-            nc.scalar.copy(
-                res_bf[c][:].rearrange("p (n i t) -> p n t i", i=4, t=PACK), res[c][:].rearrange("p t (n i) -> p n t i", i=4)
-            )
-            nc.vector.quantize_mx(out=res_codes[c][:].bitcast(FP8X4), scales=res_sc[:, CH * c : CH * (c + 1)], in_=res_bf[c][:])
-            nc.sync.dma_start(out=words_v[:, CH * c : CH * (c + 1)], in_=res_codes[c][:].bitcast(I32))
+        def stage_mix(c, parts):
+            for cols in parts:
+                nc.vector.tensor_tensor(prod[c][:, :, cols], gate[c][:, :, cols], diff[c][:, :, cols], MULT)
+            for cols in parts:
+                nc.vector.tensor_tensor(res[c][:, :, cols], prod[c][:, :, cols], skip_of(c)[:, :, cols], ADD)
 
-        for step in range(NCH + 2):
-            if step < NCH:
-                stage_gate(step)
-            if 1 <= step <= NCH:
-                stage_mix(step - 1)
-            if step >= 2:
-                stage_planes(step - 2)
+        def stage_out(i, parts):
+            j0, j1 = CH * spans[i][0], CH * spans[i][1]
+            nc.sync.dma_start(out=out_v[:, :, j0:j1], in_=res_t[i][:])
+            for cols in parts:
+                packed = res_bf[i][:, PACK * cols.start : PACK * cols.stop]
+                nc.scalar.copy(
+                    packed.rearrange("p (n i t) -> p n t i", i=4, t=PACK), res_t[i][:, :, cols].rearrange("p t (n i) -> p n t i", i=4)
+                )
+                nc.vector.quantize_mx(
+                    out=res_codes[i][:, cols].bitcast(FP8X4),
+                    scales=res_sc[:, j0 + cols.start : j0 + cols.stop],
+                    in_=packed,
+                )
+            nc.sync.dma_start(out=words_v[:, j0:j1], in_=res_codes[i][:].bitcast(I32))
+
+        whole = [slice(0, CH)]
+        halves = [slice(0, CH // 2), slice(CH // 2, CH)]
+        for c in range(NCH):
+            stage_gate(c)
+            stage_diff(c)
+        stage_mix(0, whole)
+        stage_mix(1, whole)
+        stage_out(0, [slice(0, 2 * CH)])
+        stage_mix(2, whole)
+        stage_out(1, whole)
+        stage_mix(3, halves)
+        stage_out(2, halves)
         for q in range(4):
             eng = nc.sync if q % 2 == 0 else nc.scalar
             eng.dma_start(out=out_2[0, 4 * q : 4 * q + 4, :].bitcast(I32), in_=res_sc[32 * q : 32 * q + 4, :].bitcast(I32))

@@ -24,7 +24,7 @@ KP = P * PACK
 CH = 128
 NCH = S // CH
 LC = CH // 16
-V_SHARE_M = 40
+V_SHARE = (32, 32, 32, 48)
 
 
 def tile_picked_zhwy_lin_po_kernel(
@@ -41,7 +41,7 @@ def tile_picked_zhwy_lin_po_kernel(
         offs_sb = keep.tile([P, S // 16], U16, name="offs_sb")
         tok_sb = keep.tile([P, S // 16], U16, name="tok_sb")
 
-        xs_win = sb("xs_win", [P, T], U8)
+        xs_win = keep.tile([P, T], U8, name="xs_win", tag="xs_slot", align_bytes=64)
         es_win = keep.tile([P, T], U8, name="es_win", tag="es_slot", align_bytes=64)
         w3s_raw = keep.tile([P, H], U8, name="w3s_raw", tag="w3s_slot", align_bytes=64)
         table_in = sb("table_in", [P, 1], F32)
@@ -54,7 +54,7 @@ def tile_picked_zhwy_lin_po_kernel(
 
         w_src = [w1[0:KP, :], w1[KP:K, :], w2[0:KP, :], w2[KP:K, :]]
         w_raw = [sb(f"w_raw{g}", [P, PACK, H], F32) for g in range(4)]
-        x_win = [sb(f"x_win{g}", [P, T], U32) for g in range(2)]
+        x_win = [keep.tile([P, T], U32, name=f"x_win{g}", tag=f"x_slot{g}", align_bytes=64) for g in range(2)]
         e_win = sb("e_win", [P, 2, T], U32)
 
         def load_w(g):
@@ -78,8 +78,8 @@ def tile_picked_zhwy_lin_po_kernel(
         load_w(1)
         for q in range(4):
             nc.sync.dma_start(out=w3s_raw[32 * q : 32 * q + 4, :].bitcast(I32), in_=w3_scales[0, 4 * q : 4 * q + 4, :].bitcast(I32))
-        load_w(2)
         load_x(0)
+        load_w(2)
         nc.sync.dma_start(tok_sb[:], tok)
         load_planes(es_win, e_scales)
         load_w(3)
@@ -89,8 +89,9 @@ def tile_picked_zhwy_lin_po_kernel(
             nc.sync.dma_start(out=skip_sb[a][:], in_=skip_v[:, :, 2 * CH * a : 2 * CH * (a + 1)])
 
         w_bf = [sb(f"w_bf{g}", [P, PACK * H], BF16) for g in range(4)]
-        w_codes = [sb(f"w_codes{g}", [P, H], U32) for g in range(4)]
-        sc_tags = ["w_sc0", "w3s_slot", "es_slot", "w_sc3"]
+        code_tags = ["w_codes0", "x_slot0", "w_codes2", "w_codes3"]
+        w_codes = []
+        sc_tags = ["xs_slot", "w3s_slot", "es_slot", "w_sc3"]
         w_sc = []
         x_picked = [sb(f"x_picked{g}", [P, S], U32) for g in range(2)]
         e_spans = [(0, 1), (1, 2), (2, 4)]
@@ -101,12 +102,14 @@ def tile_picked_zhwy_lin_po_kernel(
         w3_dealt = sb("w3_dealt", [P, 2 * H], U8)
         w3s_dealt = sb("w3s_dealt", [P, H], U8)
 
-        def cast_views(g):
+        def cast_w(g):
             dst = w_bf[g][:].rearrange("p (t m j) -> p m j t", t=PACK, j=PACK)
             src = w_raw[g][:].rearrange("p j (m t) -> p m j t", t=PACK)
-            return dst, src
+            nc.vector.tensor_copy(dst[:, : V_SHARE[g]], src[:, : V_SHARE[g]])
+            nc.scalar.copy(dst[:, V_SHARE[g] :], src[:, V_SHARE[g] :])
 
         def quant_w(g):
+            w_codes.append(keep.tile([P, H], U32, name=f"w_codes{g}", tag=code_tags[g], align_bytes=64))
             w_sc.append(keep.tile([P, H], U8, name=f"w_sc{g}", tag=sc_tags[g], align_bytes=64))
             nc.vector.quantize_mx(out=w_codes[g][:].bitcast(FP8X4), scales=w_sc[g][:], in_=w_bf[g][:])
 
@@ -149,21 +152,16 @@ def tile_picked_zhwy_lin_po_kernel(
         nc.vector.tensor_copy(
             w3_dealt[:].rearrange("p (t m b) -> p t m b", t=PACK, b=2), w3_raw[:].rearrange("p (m t b) -> p t m b", t=PACK, b=2)
         )
-        dst, src = cast_views(0)
-        nc.scalar.copy(dst, src)
+        cast_w(0)
         quant_w(0)
-        dst, src = cast_views(1)
-        nc.scalar.copy(dst, src)
+        cast_w(1)
         nc.vector.tensor_copy(w3s_dealt[:].rearrange("p (t m) -> p t m", t=PACK), w3s_raw[:].rearrange("p (m t) -> p t m", t=PACK))
-        quant_w(1)
-        dst, src = cast_views(2)
-        nc.scalar.copy(dst, src)
         gather_x(0)
+        quant_w(1)
+        cast_w(2)
         nc.vector.tensor_copy(es_picked[:], es_win[:].indirect(tok_sb[:]))
         quant_w(2)
-        dst, src = cast_views(3)
-        nc.vector.tensor_copy(dst[:, :V_SHARE_M], src[:, :V_SHARE_M])
-        nc.scalar.copy(dst[:, V_SHARE_M:], src[:, V_SHARE_M:])
+        cast_w(3)
         gather_x(1)
         quant_w(3)
         for rep in range(3):

@@ -23,8 +23,7 @@ PACK = 4
 KP = P * PACK
 CH = 128
 NCH = S // CH
-LC = CH // 16
-V_SHARE = (32, 32, 32, 48)
+V_SHARE = (32, 32, 32, 24, 32)
 
 
 def tile_picked_zhwy_lin_po_kernel(
@@ -41,9 +40,9 @@ def tile_picked_zhwy_lin_po_kernel(
         offs_sb = keep.tile([P, S // 16], U16, name="offs_sb")
         tok_sb = keep.tile([P, S // 16], U16, name="tok_sb")
 
-        xs_win = keep.tile([P, T], U8, name="xs_win", tag="xs_slot", align_bytes=64)
-        es_win = keep.tile([P, T], U8, name="es_win", tag="es_slot", align_bytes=64)
-        w3s_raw = keep.tile([P, H], U8, name="w3s_raw", tag="w3s_slot", align_bytes=64)
+        xs_win = sb("xs_win", [P, T], U8)
+        es_win = sb("es_win", [P, T], U8)
+        w3s_raw = sb("w3s_raw", [P, H], U8)
         table_in = sb("table_in", [P, 1], F32)
         table_out = sb("table_out", [P, 1], F32)
         nc.vector.memset(table_in[:], 0.0)
@@ -53,15 +52,17 @@ def tile_picked_zhwy_lin_po_kernel(
         nc.vector.memset(w3s_raw[:].bitcast(I32), 0)
 
         w_src = [w1[0:KP, :], w1[KP:K, :], w2[0:KP, :], w2[KP:K, :]]
-        w_raw = [sb(f"w_raw{g}", [P, PACK, H], F32) for g in range(4)]
-        x_win = [keep.tile([P, T], U32, name=f"x_win{g}", tag=f"x_slot{g}", align_bytes=64) for g in range(2)]
-        e_win = sb("e_win", [P, 2, T], U32)
+        pieces = [(0, 0, H), (1, 0, H), (2, 0, H), (3, 0, H // 2), (3, H // 2, H)]
+        w_raw = [sb(f"w_raw{i}", [P, PACK, c1 - c0], F32) for i, (g, c0, c1) in enumerate(pieces)]
+        tab_win = [sb(f"tab_win{g}", [P, T], U32) for g in range(4)]
+        tab_src = [x_words[0], x_words[1], e_words[0], e_words[1]]
 
-        def load_w(g):
-            nc.sync.dma_start(out=w_raw[g][:], in_=w_src[g].rearrange("(p j) c -> p j c", j=PACK))
+        def load_w(i):
+            g, c0, c1 = pieces[i]
+            nc.sync.dma_start(out=w_raw[i][:], in_=w_src[g].rearrange("(p j) c -> p j c", j=PACK)[:, :, c0:c1])
 
-        def load_x(g):
-            nc.sync.dma_start(out=x_win[g][:].bitcast(I32), in_=x_words[g].rearrange("p n t -> p (n t)").bitcast(I32))
+        def load_tab(g):
+            nc.sync.dma_start(out=tab_win[g][:].bitcast(I32), in_=tab_src[g].rearrange("p n t -> p (n t)").bitcast(I32))
 
         w3_raw = sb("w3_raw", [P, 2 * H], U8)
 
@@ -71,103 +72,103 @@ def tile_picked_zhwy_lin_po_kernel(
 
         skip_sb = [sb(f"skip{a}", [P, PACK, 2 * CH], F32) for a in range(2)]
         skip_v = skip.rearrange("(p t) j -> p t j", t=PACK)
-        load_w(0)
+        load_tab(0)
         nc.sync.dma_start(offs_sb[:], offs)
-        nc.sync.dma_start(out=w3_raw[:].bitcast(I32), in_=w3_words[0].bitcast(I32))
+        load_tab(1)
         load_planes(xs_win, x_scales)
+        load_w(0)
+        nc.sync.dma_start(out=w3_raw[:].bitcast(I32), in_=w3_words[0].bitcast(I32))
+        nc.sync.dma_start(tok_sb[:], tok)
         load_w(1)
+        load_planes(es_win, e_scales)
+        load_w(2)
+        load_tab(2)
         for q in range(4):
             nc.sync.dma_start(out=w3s_raw[32 * q : 32 * q + 4, :].bitcast(I32), in_=w3_scales[0, 4 * q : 4 * q + 4, :].bitcast(I32))
-        load_x(0)
-        load_w(2)
-        nc.sync.dma_start(tok_sb[:], tok)
-        load_planes(es_win, e_scales)
         load_w(3)
-        load_x(1)
-        nc.sync.dma_start(out=e_win[:].bitcast(I32), in_=e_words.rearrange("o p n t -> p o (n t)").bitcast(I32))
+        load_w(4)
+        load_tab(3)
         for a in range(2):
             nc.sync.dma_start(out=skip_sb[a][:], in_=skip_v[:, :, 2 * CH * a : 2 * CH * (a + 1)])
 
-        w_bf = [sb(f"w_bf{g}", [P, PACK * H], BF16) for g in range(4)]
-        code_tags = ["w_codes0", "x_slot0", "w_codes2", "w_codes3"]
-        w_codes = []
-        sc_tags = ["xs_slot", "w3s_slot", "es_slot", "w_sc3"]
-        w_sc = []
-        x_picked = [sb(f"x_picked{g}", [P, S], U32) for g in range(2)]
-        e_spans = [(0, 1), (1, 2), (2, 4)]
-        e_tiles = [[sb(f"e_picked{g}_{a}", [P, CH * (b - a)], U32) for a, b in e_spans] for g in range(2)]
-        e_picked = [[t[0][:], t[1][:], t[2][:, 0:CH], t[2][:, CH : 2 * CH]] for t in e_tiles]
+        w_bf = [sb(f"w_bf{i}", [P, PACK * (c1 - c0)], BF16) for i, (g, c0, c1) in enumerate(pieces)]
+        w_codes = [sb(f"w_codes{g}", [P, H], U32) for g in range(4)]
+        w_sc = [sb(f"w_sc{g}", [P, H], U8) for g in range(4)]
+        picked = [sb(f"picked{g}", [P, S], U32) for g in range(3)]
+        last_spans = [(0, 1), (1, 2), (2, 4)]
+        last_tiles = [sb(f"picked3_{a}", [P, CH * (b - a)], U32) for a, b in last_spans]
+        last_picked = [last_tiles[0][:], last_tiles[1][:], last_tiles[2][:, 0:CH], last_tiles[2][:, CH : 2 * CH]]
         xs_picked = sb("xs_picked", [P, S], U8)
         es_picked = sb("es_picked", [P, S], U8)
         w3_dealt = sb("w3_dealt", [P, 2 * H], U8)
         w3s_dealt = sb("w3s_dealt", [P, H], U8)
 
-        def cast_w(g):
-            dst = w_bf[g][:].rearrange("p (t m j) -> p m j t", t=PACK, j=PACK)
-            src = w_raw[g][:].rearrange("p j (m t) -> p m j t", t=PACK)
-            nc.vector.tensor_copy(dst[:, : V_SHARE[g]], src[:, : V_SHARE[g]])
-            nc.scalar.copy(dst[:, V_SHARE[g] :], src[:, V_SHARE[g] :])
+        def cast_w(i):
+            dst = w_bf[i][:].rearrange("p (t m j) -> p m j t", t=PACK, j=PACK)
+            src = w_raw[i][:].rearrange("p j (m t) -> p m j t", t=PACK)
+            if V_SHARE[i]:
+                nc.vector.tensor_copy(dst[:, : V_SHARE[i]], src[:, : V_SHARE[i]])
+            nc.scalar.copy(dst[:, V_SHARE[i] :], src[:, V_SHARE[i] :])
 
-        def quant_w(g):
-            w_codes.append(keep.tile([P, H], U32, name=f"w_codes{g}", tag=code_tags[g], align_bytes=64))
-            w_sc.append(keep.tile([P, H], U8, name=f"w_sc{g}", tag=sc_tags[g], align_bytes=64))
-            nc.vector.quantize_mx(out=w_codes[g][:].bitcast(FP8X4), scales=w_sc[g][:], in_=w_bf[g][:])
+        def quant_w(i):
+            g, c0, c1 = pieces[i]
+            if c1 - c0 == H:
+                nc.vector.quantize_mx(out=w_codes[g][:].bitcast(FP8X4), scales=w_sc[g][:], in_=w_bf[i][:])
+                return
+            width = c1 - c0
+            for t in range(PACK):
+                cols = slice(P * t + c0 // PACK, P * t + c1 // PACK)
+                nc.vector.quantize_mx(
+                    out=w_codes[g][:, cols].bitcast(FP8X4), scales=w_sc[g][:, cols], in_=w_bf[i][:, width * t : width * (t + 1)]
+                )
 
-        def gather_x(g):
-            nc.vector.tensor_copy(x_picked[g][:], x_win[g][:].indirect(offs_sb[:]))
-
-        def gather_e(g, c):
-            a, b = e_spans[c]
-            nc.vector.tensor_copy(e_tiles[g][c][:], e_win[:, g, :].indirect(tok_sb[:, LC * a : LC * b]))
+        def gather(g):
+            nc.vector.tensor_copy(picked[g][:], tab_win[g][:].indirect((offs_sb if g < 2 else tok_sb)[:]))
 
         h_ps = [psum.tile([P, PACK, CH], F32, name=f"h_ps{c}") for c in range(NCH)]
         u_ps = [psum.tile([P, PACK, CH], F32, name=f"u_ps{c}") for c in range(NCH)]
 
-        def h_pass(c, t, g):
-            cols = slice(CH * c, CH * (c + 1))
-            mc = slice(P * t, P * (t + 1))
+        def h_passes(g):
             planes = xs_picked if g < 2 else es_picked
-            nc.tensor.matmul_mx(
-                out=h_ps[c][:, t, :],
-                lhsT=w_codes[g][:, mc].bitcast(FP8X4),
-                lhsT_scale=w_sc[g][:, mc],
-                rhs=(x_picked[g][:, cols] if g < 2 else e_picked[g - 2][c]).bitcast(FP8X4),
-                rhs_scale=planes[4 * (g % 2) : P, cols],
-                start=(g == 0),
-                stop=(g == 3),
-            )
+            for c in range(NCH):
+                cols = slice(CH * c, CH * (c + 1))
+                for t in range(PACK):
+                    mc = slice(P * t, P * (t + 1))
+                    nc.tensor.matmul_mx(
+                        out=h_ps[c][:, t, :],
+                        lhsT=w_codes[g][:, mc].bitcast(FP8X4),
+                        lhsT_scale=w_sc[g][:, mc],
+                        rhs=(picked[g][:, cols] if g < 3 else last_picked[c]).bitcast(FP8X4),
+                        rhs_scale=planes[4 * (g % 2) : P, cols],
+                        start=(g == 0 and t == 0),
+                        stop=(g == 3 and t == PACK - 1),
+                    )
 
-        def warm_up(g, codes, planes):
-            nc.tensor.matmul_mx(
-                out=u_ps[NCH - 1][:].rearrange("p t n -> p (t n)"),
-                lhsT=w_codes[g][:, 0:P].bitcast(FP8X4),
-                lhsT_scale=w_sc[g][:, 0:P],
-                rhs=codes[:].bitcast(FP8X4),
-                rhs_scale=planes[:],
-                start=True,
-                stop=True,
-            )
-
+        gather(0)
+        gather(1)
         nc.vector.tensor_copy(xs_picked[:], xs_win[:].indirect(offs_sb[:]))
+        cast_w(0)
         nc.vector.tensor_copy(
             w3_dealt[:].rearrange("p (t m b) -> p t m b", t=PACK, b=2), w3_raw[:].rearrange("p (m t b) -> p t m b", t=PACK, b=2)
         )
-        cast_w(0)
         quant_w(0)
+        h_passes(0)
         cast_w(1)
-        nc.vector.tensor_copy(w3s_dealt[:].rearrange("p (t m) -> p t m", t=PACK), w3s_raw[:].rearrange("p (m t) -> p t m", t=PACK))
-        gather_x(0)
-        quant_w(1)
-        cast_w(2)
         nc.vector.tensor_copy(es_picked[:], es_win[:].indirect(tok_sb[:]))
+        quant_w(1)
+        h_passes(1)
+        cast_w(2)
+        gather(2)
         quant_w(2)
+        h_passes(2)
+        nc.vector.tensor_copy(w3s_dealt[:].rearrange("p (t m) -> p t m", t=PACK), w3s_raw[:].rearrange("p (m t) -> p t m", t=PACK))
         cast_w(3)
-        gather_x(1)
         quant_w(3)
-        for rep in range(3):
-            warm_up(2, x_picked[0], xs_picked)
-        for rep in range(2):
-            warm_up(0, x_picked[1], xs_picked)
+        cast_w(4)
+        quant_w(4)
+        for i, (a, b) in enumerate(last_spans):
+            nc.vector.tensor_copy(last_tiles[i][:], tab_win[3][:].indirect(tok_sb[:, CH // 16 * a : CH // 16 * b]))
+        h_passes(3)
 
         h_bf = [sb(f"h_bf{c}", [P, CH * PACK], BF16) for c in range(NCH)]
         h_codes = [sb(f"h_codes{c}", [P, CH], U32) for c in range(NCH)]
@@ -175,9 +176,9 @@ def tile_picked_zhwy_lin_po_kernel(
         gate = [sb(f"gate{c}", [P, PACK, CH], F32) for c in range(NCH)]
         diff = [sb(f"diff{c}", [P, PACK, CH], F32) for c in range(NCH)]
         prod = [sb(f"prod{c}", [P, PACK, CH], F32) for c in range(NCH)]
-        spans = [(0, 2), (2, 3), (3, 4)]
+        spans = [(c, c + 1) for c in range(NCH)]
         res_t = [sb(f"res{i}", [P, PACK, CH * (b - a)], F32) for i, (a, b) in enumerate(spans)]
-        res = [res_t[0][:, :, 0:CH], res_t[0][:, :, CH : 2 * CH], res_t[1][:], res_t[2][:]]
+        res = [r[:] for r in res_t]
         res_bf = [sb(f"res_bf{i}", [P, CH * PACK * (b - a)], BF16) for i, (a, b) in enumerate(spans)]
         res_codes = [sb(f"res_codes{i}", [P, CH * (b - a)], U32) for i, (a, b) in enumerate(spans)]
         res_sc = sb("res_sc", [P, S], U8)
@@ -188,12 +189,6 @@ def tile_picked_zhwy_lin_po_kernel(
             return skip_sb[c // 2][:, :, CH * (c % 2) : CH * (c % 2 + 1)]
 
         def stage_gate(c):
-            if c < len(e_spans):
-                gather_e(0, c)
-                gather_e(1, c)
-            for t in range(PACK):
-                for g in range(4):
-                    h_pass(c, t, g)
             nc.scalar.copy(h_bf[c][:].rearrange("p (n t) -> p n t", t=PACK), h_ps[c][:].rearrange("p t n -> p n t"))
             nc.vector.quantize_mx(out=h_codes[c][:].bitcast(FP8X4), scales=h_sc[c][:], in_=h_bf[c][:])
             for t in range(PACK):
@@ -236,14 +231,11 @@ def tile_picked_zhwy_lin_po_kernel(
         halves = [slice(0, CH // 2), slice(CH // 2, CH)]
         for c in range(NCH):
             stage_gate(c)
+        for c in range(NCH):
+            parts = whole if c < NCH - 1 else halves
             stage_diff(c)
-        stage_mix(0, whole)
-        stage_mix(1, whole)
-        stage_out(0, [slice(0, 2 * CH)])
-        stage_mix(2, whole)
-        stage_out(1, whole)
-        stage_mix(3, halves)
-        stage_out(2, halves)
+            stage_mix(c, parts)
+            stage_out(c, parts)
         for q in range(4):
             eng = nc.sync if q % 2 == 0 else nc.scalar
             eng.dma_start(out=out_2[0, 4 * q : 4 * q + 4, :].bitcast(I32), in_=res_sc[32 * q : 32 * q + 4, :].bitcast(I32))

@@ -23,7 +23,7 @@ PACK = 4
 KP = P * PACK
 CH = 128
 NCH = S // CH
-V_SHARE = (32, 32, 32, 24, 32)
+V_SHARE = (32, 16, 64, 32, 40)
 
 
 def tile_picked_zhwy_lin_po_kernel(
@@ -34,8 +34,8 @@ def tile_picked_zhwy_lin_po_kernel(
         keep = ctx.enter_context(tc.tile_pool(name="keep", bufs=1))
         psum = ctx.enter_context(tc.psum_pool(name="psum", bufs=1))
 
-        def sb(name, shape, dtype):
-            return keep.tile(shape, dtype, name=name, align_bytes=64)
+        def sb(name, shape, dtype, tag=None):
+            return keep.tile(shape, dtype, name=name, tag=tag or name, align_bytes=64)
 
         offs_sb = keep.tile([P, S // 16], U16, name="offs_sb")
         tok_sb = keep.tile([P, S // 16], U16, name="tok_sb")
@@ -48,7 +48,7 @@ def tile_picked_zhwy_lin_po_kernel(
         nc.vector.memset(table_in[:], 0.0)
         nc.scalar.activation(table_out[:], table_in[:], SIGMOID)
         nc.vector.memset(xs_win[:].bitcast(I32), 0)
-        nc.vector.memset(es_win[:].bitcast(I32), 0)
+        nc.gpsimd.memset(es_win[:].bitcast(I32), 0)
         nc.vector.memset(w3s_raw[:].bitcast(I32), 0)
 
         w_src = [w1[0:KP, :], w1[KP:K, :], w2[0:KP, :], w2[KP:K, :]]
@@ -66,25 +66,25 @@ def tile_picked_zhwy_lin_po_kernel(
 
         w3_raw = sb("w3_raw", [P, 2 * H], U8)
 
-        def load_planes(dst, src):
+        def load_planes(eng, dst, src):
             for q in range(4):
-                nc.sync.dma_start(out=dst[32 * q : 32 * q + 8, :].bitcast(I32), in_=src[:, 4 * q : 4 * q + 4, :].bitcast(I32))
+                eng.dma_start(out=dst[32 * q : 32 * q + 8, :].bitcast(I32), in_=src[:, 4 * q : 4 * q + 4, :].bitcast(I32))
 
         skip_sb = [sb(f"skip{a}", [P, PACK, 2 * CH], F32) for a in range(2)]
         skip_v = skip.rearrange("(p t) j -> p t j", t=PACK)
         load_tab(0)
         nc.sync.dma_start(offs_sb[:], offs)
+        load_planes(nc.sync, xs_win, x_scales)
         load_tab(1)
-        load_planes(xs_win, x_scales)
         load_w(0)
         nc.sync.dma_start(out=w3_raw[:].bitcast(I32), in_=w3_words[0].bitcast(I32))
         nc.sync.dma_start(tok_sb[:], tok)
+        load_planes(nc.gpsimd, es_win, e_scales)
         load_w(1)
-        load_planes(es_win, e_scales)
-        load_w(2)
         load_tab(2)
         for q in range(4):
             nc.sync.dma_start(out=w3s_raw[32 * q : 32 * q + 4, :].bitcast(I32), in_=w3_scales[0, 4 * q : 4 * q + 4, :].bitcast(I32))
+        load_w(2)
         load_w(3)
         load_w(4)
         load_tab(3)
@@ -99,9 +99,7 @@ def tile_picked_zhwy_lin_po_kernel(
         last_tiles = [sb(f"picked3_{a}", [P, CH * (b - a)], U32) for a, b in last_spans]
         last_picked = [last_tiles[0][:], last_tiles[1][:], last_tiles[2][:, 0:CH], last_tiles[2][:, CH : 2 * CH]]
         xs_picked = sb("xs_picked", [P, S], U8)
-        es_picked = sb("es_picked", [P, S], U8)
         w3_dealt = sb("w3_dealt", [P, 2 * H], U8)
-        w3s_dealt = sb("w3s_dealt", [P, H], U8)
 
         def cast_w(i):
             dst = w_bf[i][:].rearrange("p (t m j) -> p m j t", t=PACK, j=PACK)
@@ -145,8 +143,8 @@ def tile_picked_zhwy_lin_po_kernel(
                     )
 
         gather(0)
-        gather(1)
         nc.vector.tensor_copy(xs_picked[:], xs_win[:].indirect(offs_sb[:]))
+        gather(1)
         cast_w(0)
         nc.vector.tensor_copy(
             w3_dealt[:].rearrange("p (t m b) -> p t m b", t=PACK, b=2), w3_raw[:].rearrange("p (m t b) -> p t m b", t=PACK, b=2)
@@ -154,14 +152,16 @@ def tile_picked_zhwy_lin_po_kernel(
         quant_w(0)
         h_passes(0)
         cast_w(1)
+        es_picked = sb("es_picked", [P, S], U8, tag="w_bf0")
         nc.vector.tensor_copy(es_picked[:], es_win[:].indirect(tok_sb[:]))
         quant_w(1)
         h_passes(1)
-        cast_w(2)
         gather(2)
+        w3s_dealt = sb("w3s_dealt", [P, H], U8)
+        nc.vector.tensor_copy(w3s_dealt[:].rearrange("p (t m) -> p t m", t=PACK), w3s_raw[:].rearrange("p (m t) -> p t m", t=PACK))
+        cast_w(2)
         quant_w(2)
         h_passes(2)
-        nc.vector.tensor_copy(w3s_dealt[:].rearrange("p (t m) -> p t m", t=PACK), w3s_raw[:].rearrange("p (m t) -> p t m", t=PACK))
         cast_w(3)
         quant_w(3)
         cast_w(4)

@@ -77,7 +77,6 @@ def tile_picked_zhwy_lin_po_kernel(
         load_planes(nc.sync, xs_win, x_scales)
         load_tab(1)
         load_w(0)
-        nc.sync.dma_start(out=w3_raw[:].bitcast(I32), in_=w3_words[0].bitcast(I32))
         nc.sync.dma_start(tok_sb[:], tok)
         load_planes(nc.gpsimd, es_win, e_scales)
         load_w(1)
@@ -88,6 +87,7 @@ def tile_picked_zhwy_lin_po_kernel(
         load_w(3)
         load_w(4)
         load_tab(3)
+        nc.sync.dma_start(out=w3_raw[:].bitcast(I32), in_=w3_words[0].bitcast(I32))
         for a in range(2):
             nc.sync.dma_start(out=skip_sb[a][:], in_=skip_v[:, :, 2 * CH * a : 2 * CH * (a + 1)])
 
@@ -146,9 +146,6 @@ def tile_picked_zhwy_lin_po_kernel(
         nc.vector.tensor_copy(xs_picked[:], xs_win[:].indirect(offs_sb[:]))
         gather(1)
         cast_w(0)
-        nc.vector.tensor_copy(
-            w3_dealt[:].rearrange("p (t m b) -> p t m b", t=PACK, b=2), w3_raw[:].rearrange("p (m t b) -> p t m b", t=PACK, b=2)
-        )
         quant_w(0)
         h_passes(0)
         cast_w(1)
@@ -168,6 +165,9 @@ def tile_picked_zhwy_lin_po_kernel(
         quant_w(4)
         for i, (a, b) in enumerate(last_spans):
             nc.vector.tensor_copy(last_tiles[i][:], tab_win[3][:].indirect(tok_sb[:, CH // 16 * a : CH // 16 * b]))
+        nc.scalar.copy(
+            w3_dealt[:].bitcast(U16).rearrange("p (t m) -> p t m", t=PACK), w3_raw[:].bitcast(U16).rearrange("p (m t) -> p t m", t=PACK)
+        )
         h_passes(3)
 
         h_bf = [sb(f"h_bf{c}", [P, CH * PACK], BF16) for c in range(NCH)]

@@ -32,6 +32,7 @@ def tile_picked_zhwy_lin_po_kernel(
     nc = tc.nc
     with ExitStack() as ctx:
         keep = ctx.enter_context(tc.tile_pool(name="keep", bufs=1))
+        late = ctx.enter_context(tc.tile_pool(name="late", bufs=1))
         psum = ctx.enter_context(tc.psum_pool(name="psum", bufs=1))
 
         def sb(name, shape, dtype, tag=None):
@@ -64,13 +65,13 @@ def tile_picked_zhwy_lin_po_kernel(
         def load_tab(g):
             nc.sync.dma_start(out=tab_win[g][:].bitcast(I32), in_=tab_src[g].rearrange("p n t -> p (n t)").bitcast(I32))
 
-        w3_raw = sb("w3_raw", [P, 2 * H], U8)
+        w3_raw = late.tile([P, 2048 * NCH + 64], U8, name="w3_raw", offset=0, align_bytes=64)[:, : 2 * H]
 
         def load_planes(eng, dst, src):
             for q in range(4):
                 eng.dma_start(out=dst[32 * q : 32 * q + 8, :].bitcast(I32), in_=src[:, 4 * q : 4 * q + 4, :].bitcast(I32))
 
-        skip_sb = [sb(f"skip{a}", [P, PACK, 2 * CH], F32) for a in range(2)]
+        skip_sb = [sb("skip0", [P, PACK, 2 * CH], F32)]
         skip_v = skip.rearrange("(p t) j -> p t j", t=PACK)
         load_tab(0)
         nc.sync.dma_start(offs_sb[:], offs)
@@ -87,9 +88,8 @@ def tile_picked_zhwy_lin_po_kernel(
         load_w(3)
         load_w(4)
         load_tab(3)
-        nc.sync.dma_start(out=w3_raw[:].bitcast(I32), in_=w3_words[0].bitcast(I32))
-        for a in range(2):
-            nc.sync.dma_start(out=skip_sb[a][:], in_=skip_v[:, :, 2 * CH * a : 2 * CH * (a + 1)])
+        nc.sync.dma_start(out=w3_raw.bitcast(I32), in_=w3_words[0].bitcast(I32))
+        nc.sync.dma_start(out=skip_sb[0][:], in_=skip_v[:, :, 0 : 2 * CH])
 
         w_bf = [sb(f"w_bf{i}", [P, PACK * (c1 - c0)], BF16) for i, (g, c0, c1) in enumerate(pieces)]
         w_codes = [sb(f"w_codes{g}", [P, H], U32) for g in range(4)]
@@ -123,8 +123,8 @@ def tile_picked_zhwy_lin_po_kernel(
         def gather(g):
             nc.vector.tensor_copy(picked[g][:], tab_win[g][:].indirect((offs_sb if g < 2 else tok_sb)[:]))
 
-        h_ps = [psum.tile([P, PACK, CH], F32, name=f"h_ps{c}") for c in range(NCH)]
-        u_ps = [psum.tile([P, PACK, CH], F32, name=f"u_ps{c}") for c in range(NCH)]
+        h_ps = [psum.tile([P, PACK, CH], F32, name=f"h_ps{c}", tag=f"h_ps{c}") for c in range(NCH)]
+        side_ps = [psum.tile([P, PACK, CH], F32, name=f"side_ps{c}", tag=f"side_ps{c}") for c in range(NCH)]
 
         def h_passes(g):
             planes = xs_picked if g < 2 else es_picked
@@ -166,11 +166,13 @@ def tile_picked_zhwy_lin_po_kernel(
         for i, (a, b) in enumerate(last_spans):
             nc.vector.tensor_copy(last_tiles[i][:], tab_win[3][:].indirect(tok_sb[:, CH // 16 * a : CH // 16 * b]))
         nc.scalar.copy(
-            w3_dealt[:].bitcast(U16).rearrange("p (t m) -> p t m", t=PACK), w3_raw[:].bitcast(U16).rearrange("p (m t) -> p t m", t=PACK)
+            w3_dealt[:].bitcast(U16).rearrange("p (t m) -> p t m", t=PACK), w3_raw.bitcast(U16).rearrange("p (m t) -> p t m", t=PACK)
         )
+        skip_sb.append(late.tile([P, PACK, 2 * CH], F32, name="skip1", offset=2048 * NCH, align_bytes=64))
+        nc.scalar.dma_start(out=skip_sb[1][:], in_=skip_v[:, :, 2 * CH : S])
         h_passes(3)
 
-        h_bf = [sb(f"h_bf{c}", [P, CH * PACK], BF16) for c in range(NCH)]
+        h_bf = [late.tile([P, CH * PACK], BF16, name=f"h_bf{c}", offset=2048 * c, align_bytes=64) for c in range(NCH)]
         h_codes = [sb(f"h_codes{c}", [P, CH], U32) for c in range(NCH)]
         h_sc = [sb(f"h_sc{c}", [P, CH], U8) for c in range(NCH)]
         gate = [sb(f"gate{c}", [P, PACK, CH], F32) for c in range(NCH)]
@@ -180,7 +182,7 @@ def tile_picked_zhwy_lin_po_kernel(
         res_t = [sb(f"res{i}", [P, PACK, CH * (b - a)], F32) for i, (a, b) in enumerate(spans)]
         res = [r[:] for r in res_t]
         res_bf = [sb(f"res_bf{i}", [P, CH * PACK * (b - a)], BF16) for i, (a, b) in enumerate(spans)]
-        res_codes = [sb(f"res_codes{i}", [P, CH * (b - a)], U32) for i, (a, b) in enumerate(spans)]
+        res_codes = [sb(f"res_codes{a}", [P, 2 * CH], U32) for a in range(2)]
         res_sc = sb("res_sc", [P, S], U8)
         out_v = out_0.rearrange("(p t) j -> p t j", t=PACK)
         words_v = out_1[0].rearrange("p n t -> p (n t)").bitcast(I32)
@@ -188,12 +190,14 @@ def tile_picked_zhwy_lin_po_kernel(
         def skip_of(c):
             return skip_sb[c // 2][:, :, CH * (c % 2) : CH * (c % 2 + 1)]
 
-        def stage_gate(c):
+        def leave_psum(c):
             nc.scalar.copy(h_bf[c][:].rearrange("p (n t) -> p n t", t=PACK), h_ps[c][:].rearrange("p t n -> p n t"))
+
+        def stage_gate(c):
             nc.vector.quantize_mx(out=h_codes[c][:].bitcast(FP8X4), scales=h_sc[c][:], in_=h_bf[c][:])
             for t in range(PACK):
                 nc.tensor.matmul_mx(
-                    out=u_ps[c][:, t, :],
+                    out=side_ps[c][:, t, :],
                     lhsT=w3_dealt[:, 2 * P * t : 2 * P * (t + 1)].bitcast(FP4X4),
                     lhsT_scale=w3s_dealt[:, P * t : P * (t + 1)],
                     rhs=h_codes[c][:].bitcast(FP8X4),
@@ -201,41 +205,64 @@ def tile_picked_zhwy_lin_po_kernel(
                     start=True,
                     stop=True,
                 )
-            nc.scalar.activation(gate[c][:], u_ps[c][:], SIGMOID)
+            nc.scalar.activation(gate[c][:], side_ps[c][:], SIGMOID)
 
         def stage_diff(c):
             nc.vector.tensor_tensor(diff[c][:], h_ps[c][:], skip_of(c), SUB)
 
-        def stage_mix(c, parts):
+        def stage_mul(c, parts):
             for cols in parts:
                 nc.vector.tensor_tensor(prod[c][:, :, cols], gate[c][:, :, cols], diff[c][:, :, cols], MULT)
+
+        def stage_add(c, parts):
             for cols in parts:
                 nc.vector.tensor_tensor(res[c][:, :, cols], prod[c][:, :, cols], skip_of(c)[:, :, cols], ADD)
 
-        def stage_out(i, parts):
-            j0, j1 = CH * spans[i][0], CH * spans[i][1]
-            nc.sync.dma_start(out=out_v[:, :, j0:j1], in_=res_t[i][:])
-            for cols in parts:
-                packed = res_bf[i][:, PACK * cols.start : PACK * cols.stop]
-                nc.scalar.copy(
-                    packed.rearrange("p (n i t) -> p n t i", i=4, t=PACK), res_t[i][:, :, cols].rearrange("p t (n i) -> p n t i", i=4)
-                )
-                nc.vector.quantize_mx(
-                    out=res_codes[i][:, cols].bitcast(FP8X4),
-                    scales=res_sc[:, j0 + cols.start : j0 + cols.stop],
-                    in_=packed,
-                )
-            nc.sync.dma_start(out=words_v[:, j0:j1], in_=res_codes[i][:].bitcast(I32))
+        def store_res(c):
+            nc.sync.dma_start(out=out_v[:, :, CH * c : CH * (c + 1)], in_=res_t[c][:])
+
+        def round_res(c, cols, on_vector=False):
+            dst = res_bf[c][:, PACK * cols.start : PACK * cols.stop].rearrange("p (n i t) -> p n t i", i=4, t=PACK)
+            src = res_t[c][:, :, cols].rearrange("p t (n i) -> p n t i", i=4)
+            if on_vector:
+                nc.vector.tensor_copy(dst, src)
+            else:
+                nc.scalar.copy(dst, src)
+
+        def quant_res(c, cols):
+            nc.vector.quantize_mx(
+                out=res_codes[c // 2][:, CH * (c % 2) + cols.start : CH * (c % 2) + cols.stop].bitcast(FP8X4),
+                scales=res_sc[:, CH * c + cols.start : CH * c + cols.stop],
+                in_=res_bf[c][:, PACK * cols.start : PACK * cols.stop],
+            )
+
 
         whole = [slice(0, CH)]
         halves = [slice(0, CH // 2), slice(CH // 2, CH)]
         for c in range(NCH):
-            stage_gate(c)
+            leave_psum(c)
         for c in range(NCH):
-            parts = whole if c < NCH - 1 else halves
+            stage_gate(c)
             stage_diff(c)
-            stage_mix(c, parts)
-            stage_out(c, parts)
+        stage_mul(0, whole)
+        for c in range(NCH - 1):
+            if c + 1 < NCH - 1:
+                stage_mul(c + 1, whole)
+            stage_add(c, whole)
+            store_res(c)
+            round_res(c, whole[0])
+        stage_mul(3, halves)
+        stage_add(3, halves)
+        store_res(3)
+        round_res(3, halves[0])
+        quant_res(0, whole[0])
+        round_res(3, halves[1], on_vector=True)
+        quant_res(1, whole[0])
+        nc.sync.dma_start(out=words_v[:, : 2 * CH], in_=res_codes[0][:].bitcast(I32))
+        quant_res(2, whole[0])
+        for cols in halves:
+            quant_res(3, cols)
+        nc.sync.dma_start(out=words_v[:, 2 * CH :], in_=res_codes[1][:].bitcast(I32))
         for q in range(4):
             eng = nc.sync if q % 2 == 0 else nc.scalar
             eng.dma_start(out=out_2[0, 4 * q : 4 * q + 4, :].bitcast(I32), in_=res_sc[32 * q : 32 * q + 4, :].bitcast(I32))

@@ -32,7 +32,6 @@ def tile_picked_zhwy_lin_po_kernel(
     nc = tc.nc
     with ExitStack() as ctx:
         keep = ctx.enter_context(tc.tile_pool(name="keep", bufs=1))
-        late = ctx.enter_context(tc.tile_pool(name="late", bufs=1))
         psum = ctx.enter_context(tc.psum_pool(name="psum", bufs=1))
 
         def sb(name, shape, dtype, tag=None):
@@ -65,13 +64,13 @@ def tile_picked_zhwy_lin_po_kernel(
         def load_tab(g):
             nc.sync.dma_start(out=tab_win[g][:].bitcast(I32), in_=tab_src[g].rearrange("p n t -> p (n t)").bitcast(I32))
 
-        w3_raw = late.tile([P, 2048 * NCH + 64], U8, name="w3_raw", offset=0, align_bytes=64)[:, : 2 * H]
+        w3_raw = sb("w3_raw", [P, 2 * H], U8)[:]
 
         def load_planes(eng, dst, src):
             for q in range(4):
                 eng.dma_start(out=dst[32 * q : 32 * q + 8, :].bitcast(I32), in_=src[:, 4 * q : 4 * q + 4, :].bitcast(I32))
 
-        skip_sb = [sb("skip0", [P, PACK, 2 * CH], F32)]
+        skip_sb = [sb(f"skip{a}", [P, PACK, 2 * CH], F32) for a in range(2)]
         skip_v = skip.rearrange("(p t) j -> p t j", t=PACK)
         load_tab(0)
         nc.sync.dma_start(offs_sb[:], offs)
@@ -89,7 +88,8 @@ def tile_picked_zhwy_lin_po_kernel(
         load_w(4)
         load_tab(3)
         nc.sync.dma_start(out=w3_raw.bitcast(I32), in_=w3_words[0].bitcast(I32))
-        nc.sync.dma_start(out=skip_sb[0][:], in_=skip_v[:, :, 0 : 2 * CH])
+        for a in range(2):
+            nc.sync.dma_start(out=skip_sb[a][:], in_=skip_v[:, :, 2 * CH * a : 2 * CH * (a + 1)])
 
         w_bf = [sb(f"w_bf{i}", [P, PACK * (c1 - c0)], BF16) for i, (g, c0, c1) in enumerate(pieces)]
         w_codes = [sb(f"w_codes{g}", [P, H], U32) for g in range(4)]
@@ -165,14 +165,12 @@ def tile_picked_zhwy_lin_po_kernel(
         quant_w(4)
         for i, (a, b) in enumerate(last_spans):
             nc.vector.tensor_copy(last_tiles[i][:], tab_win[3][:].indirect(tok_sb[:, CH // 16 * a : CH // 16 * b]))
-        nc.scalar.copy(
-            w3_dealt[:].bitcast(U16).rearrange("p (t m) -> p t m", t=PACK), w3_raw.bitcast(U16).rearrange("p (m t) -> p t m", t=PACK)
+        nc.vector.tensor_copy(
+            w3_dealt[:].rearrange("p (t m b) -> p t m b", t=PACK, b=2), w3_raw.rearrange("p (m t b) -> p t m b", t=PACK, b=2)
         )
-        skip_sb.append(late.tile([P, PACK, 2 * CH], F32, name="skip1", offset=2048 * NCH, align_bytes=64))
-        nc.scalar.dma_start(out=skip_sb[1][:], in_=skip_v[:, :, 2 * CH : S])
         h_passes(3)
 
-        h_bf = [late.tile([P, CH * PACK], BF16, name=f"h_bf{c}", offset=2048 * c, align_bytes=64) for c in range(NCH)]
+        h_bf = [sb(f"h_bf{c}", [P, CH * PACK], BF16) for c in range(NCH)]
         h_codes = [sb(f"h_codes{c}", [P, CH], U32) for c in range(NCH)]
         h_sc = [sb(f"h_sc{c}", [P, CH], U8) for c in range(NCH)]
         gate = [sb(f"gate{c}", [P, PACK, CH], F32) for c in range(NCH)]

@@ -23,7 +23,7 @@ PACK = 4
 KP = P * PACK
 CH = 128
 NCH = S // CH
-V_SHARE = (32, 16, 64, 32, 40)
+V_SHARE = (0, 0, 80, 16, 40)
 
 
 def tile_picked_zhwy_lin_po_kernel(
@@ -42,20 +42,21 @@ def tile_picked_zhwy_lin_po_kernel(
 
         xs_win = sb("xs_win", [P, T], U8)
         es_win = sb("es_win", [P, T], U8)
-        w3s_raw = sb("w3s_raw", [P, H], U8)
-        table_in = sb("table_in", [P, 1], F32)
+        w3s_raw = sb("w3s_raw", [P, H + 4], U8)
         table_out = sb("table_out", [P, 1], F32)
-        nc.vector.memset(table_in[:], 0.0)
-        nc.scalar.activation(table_out[:], table_in[:], SIGMOID)
         nc.vector.memset(xs_win[:].bitcast(I32), 0)
         nc.gpsimd.memset(es_win[:].bitcast(I32), 0)
         nc.vector.memset(w3s_raw[:].bitcast(I32), 0)
+        nc.scalar.activation(table_out[:], w3s_raw[:, H : H + 4].bitcast(F32), SIGMOID)
 
         w_src = [w1[0:KP, :], w1[KP:K, :], w2[0:KP, :], w2[KP:K, :]]
         pieces = [(0, 0, H), (1, 0, H), (2, 0, H), (3, 0, H // 2), (3, H // 2, H)]
         w_raw = [sb(f"w_raw{i}", [P, PACK, c1 - c0], F32) for i, (g, c0, c1) in enumerate(pieces)]
         tab_win = [sb(f"tab_win{g}", [P, T], U32) for g in range(4)]
         tab_src = [x_words[0], x_words[1], e_words[0], e_words[1]]
+        w3_raw = sb("w3_raw", [P, 2 * H], U8)
+        skip_sb = [sb(f"skip{a}", [P, PACK, 2 * CH], F32) for a in range(2)]
+        skip_v = skip.rearrange("(p t) j -> p t j", t=PACK)
 
         def load_w(i):
             g, c0, c1 = pieces[i]
@@ -64,34 +65,30 @@ def tile_picked_zhwy_lin_po_kernel(
         def load_tab(g):
             nc.sync.dma_start(out=tab_win[g][:].bitcast(I32), in_=tab_src[g].rearrange("p n t -> p (n t)").bitcast(I32))
 
-        w3_raw = sb("w3_raw", [P, 2 * H], U8)[:]
-
         def load_planes(eng, dst, src):
             for q in range(4):
                 eng.dma_start(out=dst[32 * q : 32 * q + 8, :].bitcast(I32), in_=src[:, 4 * q : 4 * q + 4, :].bitcast(I32))
 
-        skip_sb = [sb(f"skip{a}", [P, PACK, 2 * CH], F32) for a in range(2)]
-        skip_v = skip.rearrange("(p t) j -> p t j", t=PACK)
         load_tab(0)
         nc.sync.dma_start(offs_sb[:], offs)
         load_planes(nc.sync, xs_win, x_scales)
-        load_tab(1)
         load_w(0)
+        load_tab(1)
         nc.sync.dma_start(tok_sb[:], tok)
         load_planes(nc.gpsimd, es_win, e_scales)
         load_w(1)
         load_tab(2)
         for q in range(4):
-            nc.sync.dma_start(out=w3s_raw[32 * q : 32 * q + 4, :].bitcast(I32), in_=w3_scales[0, 4 * q : 4 * q + 4, :].bitcast(I32))
+            nc.sync.dma_start(out=w3s_raw[32 * q : 32 * q + 4, :H].bitcast(I32), in_=w3_scales[0, 4 * q : 4 * q + 4, :].bitcast(I32))
         load_w(2)
         load_w(3)
         load_w(4)
         load_tab(3)
-        nc.sync.dma_start(out=w3_raw.bitcast(I32), in_=w3_words[0].bitcast(I32))
+        nc.sync.dma_start(out=w3_raw[:].bitcast(I32), in_=w3_words[0].bitcast(I32))
         for a in range(2):
             nc.sync.dma_start(out=skip_sb[a][:], in_=skip_v[:, :, 2 * CH * a : 2 * CH * (a + 1)])
 
-        w_bf = [sb(f"w_bf{i}", [P, PACK * (c1 - c0)], BF16) for i, (g, c0, c1) in enumerate(pieces)]
+        w_bf = [sb(f"w_bf{g}", [P, PACK * H], BF16) for g in range(4)]
         w_codes = [sb(f"w_codes{g}", [P, H], U32) for g in range(4)]
         w_sc = [sb(f"w_sc{g}", [P, H], U8) for g in range(4)]
         picked = [sb(f"picked{g}", [P, S], U32) for g in range(3)]
@@ -100,31 +97,24 @@ def tile_picked_zhwy_lin_po_kernel(
         last_picked = [last_tiles[0][:], last_tiles[1][:], last_tiles[2][:, 0:CH], last_tiles[2][:, CH : 2 * CH]]
         xs_picked = sb("xs_picked", [P, S], U8)
         w3_dealt = sb("w3_dealt", [P, 2 * H], U8)
+        w3s_dealt = sb("w3s_dealt", [P, H], U8)
 
-        def cast_w(i):
-            dst = w_bf[i][:].rearrange("p (t m j) -> p m j t", t=PACK, j=PACK)
+        def round_w(i):
+            g, c0, c1 = pieces[i]
+            dst = w_bf[g][:].rearrange("p (t m j) -> p m j t", t=PACK, j=PACK)[:, c0 // PACK : c1 // PACK]
             src = w_raw[i][:].rearrange("p j (m t) -> p m j t", t=PACK)
             if V_SHARE[i]:
                 nc.vector.tensor_copy(dst[:, : V_SHARE[i]], src[:, : V_SHARE[i]])
             nc.scalar.copy(dst[:, V_SHARE[i] :], src[:, V_SHARE[i] :])
 
-        def quant_w(i):
-            g, c0, c1 = pieces[i]
-            if c1 - c0 == H:
-                nc.vector.quantize_mx(out=w_codes[g][:].bitcast(FP8X4), scales=w_sc[g][:], in_=w_bf[i][:])
-                return
-            width = c1 - c0
-            for t in range(PACK):
-                cols = slice(P * t + c0 // PACK, P * t + c1 // PACK)
-                nc.vector.quantize_mx(
-                    out=w_codes[g][:, cols].bitcast(FP8X4), scales=w_sc[g][:, cols], in_=w_bf[i][:, width * t : width * (t + 1)]
-                )
+        def quant_w(g):
+            nc.vector.quantize_mx(out=w_codes[g][:].bitcast(FP8X4), scales=w_sc[g][:], in_=w_bf[g][:])
 
         def gather(g):
             nc.vector.tensor_copy(picked[g][:], tab_win[g][:].indirect((offs_sb if g < 2 else tok_sb)[:]))
 
         h_ps = [psum.tile([P, PACK, CH], F32, name=f"h_ps{c}", tag=f"h_ps{c}") for c in range(NCH)]
-        side_ps = [psum.tile([P, PACK, CH], F32, name=f"side_ps{c}", tag=f"side_ps{c}") for c in range(NCH)]
+        u_ps = [psum.tile([P, PACK, CH], F32, name=f"u_ps{c}", tag=f"u_ps{c}") for c in range(NCH)]
 
         def h_passes(g):
             planes = xs_picked if g < 2 else es_picked
@@ -144,58 +134,53 @@ def tile_picked_zhwy_lin_po_kernel(
 
         gather(0)
         nc.vector.tensor_copy(xs_picked[:], xs_win[:].indirect(offs_sb[:]))
+        round_w(0)
         gather(1)
-        cast_w(0)
         quant_w(0)
         h_passes(0)
-        cast_w(1)
+        round_w(1)
         es_picked = sb("es_picked", [P, S], U8, tag="w_bf0")
         nc.vector.tensor_copy(es_picked[:], es_win[:].indirect(tok_sb[:]))
+        gather(2)
         quant_w(1)
         h_passes(1)
-        gather(2)
-        w3s_dealt = sb("w3s_dealt", [P, H], U8)
-        nc.vector.tensor_copy(w3s_dealt[:].rearrange("p (t m) -> p t m", t=PACK), w3s_raw[:].rearrange("p (m t) -> p t m", t=PACK))
-        cast_w(2)
+        nc.vector.tensor_copy(
+            w3s_dealt[:].rearrange("p (t m) -> p t m", t=PACK), w3s_raw[:, :H].rearrange("p (m t) -> p t m", t=PACK)
+        )
+        round_w(2)
         quant_w(2)
         h_passes(2)
-        cast_w(3)
+        round_w(3)
+        round_w(4)
         quant_w(3)
-        cast_w(4)
-        quant_w(4)
         for i, (a, b) in enumerate(last_spans):
             nc.vector.tensor_copy(last_tiles[i][:], tab_win[3][:].indirect(tok_sb[:, CH // 16 * a : CH // 16 * b]))
         nc.vector.tensor_copy(
-            w3_dealt[:].rearrange("p (t m b) -> p t m b", t=PACK, b=2), w3_raw.rearrange("p (m t b) -> p t m b", t=PACK, b=2)
+            w3_dealt[:].rearrange("p (t m b) -> p t m b", t=PACK, b=2), w3_raw[:].rearrange("p (m t b) -> p t m b", t=PACK, b=2)
         )
         h_passes(3)
 
         h_bf = [sb(f"h_bf{c}", [P, CH * PACK], BF16) for c in range(NCH)]
         h_codes = [sb(f"h_codes{c}", [P, CH], U32) for c in range(NCH)]
         h_sc = [sb(f"h_sc{c}", [P, CH], U8) for c in range(NCH)]
-        gate = [sb(f"gate{c}", [P, PACK, CH], F32) for c in range(NCH)]
+        carry = [sb(f"carry{c}", [P, PACK, CH], F32) for c in range(NCH)]
         diff = [sb(f"diff{c}", [P, PACK, CH], F32) for c in range(NCH)]
         prod = [sb(f"prod{c}", [P, PACK, CH], F32) for c in range(NCH)]
-        spans = [(c, c + 1) for c in range(NCH)]
-        res_t = [sb(f"res{i}", [P, PACK, CH * (b - a)], F32) for i, (a, b) in enumerate(spans)]
-        res = [r[:] for r in res_t]
-        res_bf = [sb(f"res_bf{i}", [P, CH * PACK * (b - a)], BF16) for i, (a, b) in enumerate(spans)]
+        res = [sb(f"res{c}", [P, PACK, CH], F32) for c in range(NCH)]
+        res_bf = [sb(f"res_bf{a}", [P, 2 * CH * PACK], BF16) for a in range(2)]
         res_codes = [sb(f"res_codes{a}", [P, 2 * CH], U32) for a in range(2)]
         res_sc = sb("res_sc", [P, S], U8)
         out_v = out_0.rearrange("(p t) j -> p t j", t=PACK)
         words_v = out_1[0].rearrange("p n t -> p (n t)").bitcast(I32)
 
-        def skip_of(c):
-            return skip_sb[c // 2][:, :, CH * (c % 2) : CH * (c % 2 + 1)]
-
-        def leave_psum(c):
+        def round_h(c):
             nc.scalar.copy(h_bf[c][:].rearrange("p (n t) -> p n t", t=PACK), h_ps[c][:].rearrange("p t n -> p n t"))
 
-        def stage_gate(c):
+        def gate_product(c):
             nc.vector.quantize_mx(out=h_codes[c][:].bitcast(FP8X4), scales=h_sc[c][:], in_=h_bf[c][:])
             for t in range(PACK):
                 nc.tensor.matmul_mx(
-                    out=side_ps[c][:, t, :],
+                    out=u_ps[c][:, t, :],
                     lhsT=w3_dealt[:, 2 * P * t : 2 * P * (t + 1)].bitcast(FP4X4),
                     lhsT_scale=w3s_dealt[:, P * t : P * (t + 1)],
                     rhs=h_codes[c][:].bitcast(FP8X4),
@@ -203,63 +188,59 @@ def tile_picked_zhwy_lin_po_kernel(
                     start=True,
                     stop=True,
                 )
-            nc.scalar.activation(gate[c][:], side_ps[c][:], SIGMOID)
 
-        def stage_diff(c):
-            nc.vector.tensor_tensor(diff[c][:], h_ps[c][:], skip_of(c), SUB)
+        def carry_share(c):
+            nc.scalar.activation(carry[c][:], u_ps[c][:], SIGMOID, scale=-1.0)
 
-        def stage_mul(c, parts):
-            for cols in parts:
-                nc.vector.tensor_tensor(prod[c][:, :, cols], gate[c][:, :, cols], diff[c][:, :, cols], MULT)
+        def difference(c):
+            nc.vector.tensor_tensor(diff[c][:], skip_sb[c // 2][:, :, CH * (c % 2) : CH * (c % 2 + 1)], h_ps[c][:], SUB)
 
-        def stage_add(c, parts):
-            for cols in parts:
-                nc.vector.tensor_tensor(res[c][:, :, cols], prod[c][:, :, cols], skip_of(c)[:, :, cols], ADD)
+        def product(eng, c):
+            eng.tensor_tensor(prod[c][:], carry[c][:], diff[c][:], MULT)
 
-        def store_res(c):
-            nc.sync.dma_start(out=out_v[:, :, CH * c : CH * (c + 1)], in_=res_t[c][:])
+        def total(c):
+            nc.vector.tensor_tensor(res[c][:], h_ps[c][:], prod[c][:], ADD)
+            nc.sync.dma_start(out=out_v[:, :, CH * c : CH * (c + 1)], in_=res[c][:])
 
-        def round_res(c, cols, on_vector=False):
-            dst = res_bf[c][:, PACK * cols.start : PACK * cols.stop].rearrange("p (n i t) -> p n t i", i=4, t=PACK)
-            src = res_t[c][:, :, cols].rearrange("p t (n i) -> p n t i", i=4)
-            if on_vector:
-                nc.vector.tensor_copy(dst, src)
-            else:
-                nc.scalar.copy(dst, src)
+        def round_res(copy, c, n0, n1):
+            base = CH * (c % 2)
+            dst = res_bf[c // 2][:, PACK * (base + n0) : PACK * (base + n1)].rearrange("p (n i t) -> p n t i", i=4, t=PACK)
+            copy(dst, res[c][:, :, n0:n1].rearrange("p t (n i) -> p n t i", i=4))
 
-        def quant_res(c, cols):
+        def quant_res(c0, c1):
+            a, n0, n1 = c0 // 2, CH * (c0 % 2), CH * (c0 % 2 + c1 - c0)
             nc.vector.quantize_mx(
-                out=res_codes[c // 2][:, CH * (c % 2) + cols.start : CH * (c % 2) + cols.stop].bitcast(FP8X4),
-                scales=res_sc[:, CH * c + cols.start : CH * c + cols.stop],
-                in_=res_bf[c][:, PACK * cols.start : PACK * cols.stop],
+                out=res_codes[a][:, n0:n1].bitcast(FP8X4), scales=res_sc[:, CH * c0 : CH * c1], in_=res_bf[a][:, PACK * n0 : PACK * n1]
             )
 
-
-        whole = [slice(0, CH)]
-        halves = [slice(0, CH // 2), slice(CH // 2, CH)]
-        for c in range(NCH):
-            leave_psum(c)
-        for c in range(NCH):
-            stage_gate(c)
-            stage_diff(c)
-        stage_mul(0, whole)
-        for c in range(NCH - 1):
-            if c + 1 < NCH - 1:
-                stage_mul(c + 1, whole)
-            stage_add(c, whole)
-            store_res(c)
-            round_res(c, whole[0])
-        stage_mul(3, halves)
-        stage_add(3, halves)
-        store_res(3)
-        round_res(3, halves[0])
-        quant_res(0, whole[0])
-        round_res(3, halves[1], on_vector=True)
-        quant_res(1, whole[0])
+        for c in range(3):
+            round_h(c)
+            gate_product(c)
+            difference(c)
+        carry_share(0)
+        product(nc.gpsimd, 0)
+        round_h(3)
+        difference(3)
+        gate_product(3)
+        carry_share(1)
+        product(nc.vector, 1)
+        carry_share(2)
+        product(nc.gpsimd, 2)
+        total(0)
+        total(1)
+        carry_share(3)
+        product(nc.vector, 3)
+        round_res(nc.scalar.copy, 0, 0, CH)
+        round_res(nc.scalar.copy, 1, 0, CH)
+        total(2)
+        total(3)
+        round_res(nc.scalar.copy, 2, 0, CH)
+        round_res(nc.scalar.copy, 3, 0, CH // 2)
+        quant_res(0, 2)
         nc.sync.dma_start(out=words_v[:, : 2 * CH], in_=res_codes[0][:].bitcast(I32))
-        quant_res(2, whole[0])
-        for cols in halves:
-            quant_res(3, cols)
+        round_res(nc.vector.tensor_copy, 3, CH // 2, CH)
+        quant_res(2, 3)
+        quant_res(3, 4)
         nc.sync.dma_start(out=words_v[:, 2 * CH :], in_=res_codes[1][:].bitcast(I32))
         for q in range(4):
             eng = nc.sync if q % 2 == 0 else nc.scalar

@@ -23,7 +23,7 @@ PACK = 4
 KP = P * PACK
 CH = 128
 NCH = S // CH
-V_SHARE = (0, 0, 80, 16, 40)
+V_SHARE = (32, 16, 64, 32, 40)
 
 
 def tile_picked_zhwy_lin_po_kernel(
@@ -72,8 +72,8 @@ def tile_picked_zhwy_lin_po_kernel(
         load_tab(0)
         nc.sync.dma_start(offs_sb[:], offs)
         load_planes(nc.sync, xs_win, x_scales)
-        load_w(0)
         load_tab(1)
+        load_w(0)
         nc.sync.dma_start(tok_sb[:], tok)
         load_planes(nc.gpsimd, es_win, e_scales)
         load_w(1)
@@ -88,7 +88,7 @@ def tile_picked_zhwy_lin_po_kernel(
         for a in range(2):
             nc.sync.dma_start(out=skip_sb[a][:], in_=skip_v[:, :, 2 * CH * a : 2 * CH * (a + 1)])
 
-        w_bf = [sb(f"w_bf{g}", [P, PACK * H], BF16) for g in range(4)]
+        w_bf = [sb(f"w_bf{i}", [P, PACK * (c1 - c0)], BF16) for i, (g, c0, c1) in enumerate(pieces)]
         w_codes = [sb(f"w_codes{g}", [P, H], U32) for g in range(4)]
         w_sc = [sb(f"w_sc{g}", [P, H], U8) for g in range(4)]
         picked = [sb(f"picked{g}", [P, S], U32) for g in range(3)]
@@ -100,15 +100,23 @@ def tile_picked_zhwy_lin_po_kernel(
         w3s_dealt = sb("w3s_dealt", [P, H], U8)
 
         def round_w(i):
-            g, c0, c1 = pieces[i]
-            dst = w_bf[g][:].rearrange("p (t m j) -> p m j t", t=PACK, j=PACK)[:, c0 // PACK : c1 // PACK]
+            dst = w_bf[i][:].rearrange("p (t m j) -> p m j t", t=PACK, j=PACK)
             src = w_raw[i][:].rearrange("p j (m t) -> p m j t", t=PACK)
             if V_SHARE[i]:
                 nc.vector.tensor_copy(dst[:, : V_SHARE[i]], src[:, : V_SHARE[i]])
             nc.scalar.copy(dst[:, V_SHARE[i] :], src[:, V_SHARE[i] :])
 
-        def quant_w(g):
-            nc.vector.quantize_mx(out=w_codes[g][:].bitcast(FP8X4), scales=w_sc[g][:], in_=w_bf[g][:])
+        def quant_w(i):
+            g, c0, c1 = pieces[i]
+            width = c1 - c0
+            if width == H:
+                nc.vector.quantize_mx(out=w_codes[g][:].bitcast(FP8X4), scales=w_sc[g][:], in_=w_bf[i][:])
+                return
+            for t in range(PACK):
+                cols = slice(P * t + c0 // PACK, P * t + c1 // PACK)
+                nc.vector.quantize_mx(
+                    out=w_codes[g][:, cols].bitcast(FP8X4), scales=w_sc[g][:, cols], in_=w_bf[i][:, width * t : width * (t + 1)]
+                )
 
         def gather(g):
             nc.vector.tensor_copy(picked[g][:], tab_win[g][:].indirect((offs_sb if g < 2 else tok_sb)[:]))
@@ -134,16 +142,16 @@ def tile_picked_zhwy_lin_po_kernel(
 
         gather(0)
         nc.vector.tensor_copy(xs_picked[:], xs_win[:].indirect(offs_sb[:]))
-        round_w(0)
         gather(1)
+        round_w(0)
         quant_w(0)
         h_passes(0)
         round_w(1)
         es_picked = sb("es_picked", [P, S], U8, tag="w_bf0")
         nc.vector.tensor_copy(es_picked[:], es_win[:].indirect(tok_sb[:]))
-        gather(2)
         quant_w(1)
         h_passes(1)
+        gather(2)
         nc.vector.tensor_copy(
             w3s_dealt[:].rearrange("p (t m) -> p t m", t=PACK), w3s_raw[:, :H].rearrange("p (m t) -> p t m", t=PACK)
         )
@@ -151,8 +159,9 @@ def tile_picked_zhwy_lin_po_kernel(
         quant_w(2)
         h_passes(2)
         round_w(3)
-        round_w(4)
         quant_w(3)
+        round_w(4)
+        quant_w(4)
         for i, (a, b) in enumerate(last_spans):
             nc.vector.tensor_copy(last_tiles[i][:], tab_win[3][:].indirect(tok_sb[:, CH // 16 * a : CH // 16 * b]))
         nc.vector.tensor_copy(

@@ -23,7 +23,7 @@ PACK = 4
 KP = P * PACK
 CH = 128
 NCH = S // CH
-V_SHARE = (32, 16, 64, 32, 40)
+V_SHARE = (96, 16, 64, 32, 40)
 
 
 def tile_picked_zhwy_lin_po_kernel(

@@ -55,7 +55,7 @@ def tile_picked_zhwy_lin_po_kernel(
         tab_win = [sb(f"tab_win{g}", [P, T], U32) for g in range(4)]
         tab_src = [x_words[0], x_words[1], e_words[0], e_words[1]]
         w3_raw = sb("w3_raw", [P, 2 * H], U8)
-        skip_sb = [sb(f"skip{a}", [P, PACK, 2 * CH], F32) for a in range(2)]
+        skip_sb = [sb(f"skip{c}", [P, PACK, CH], F32) for c in range(NCH)]
         skip_v = skip.rearrange("(p t) j -> p t j", t=PACK)
 
         def load_w(i):
@@ -85,8 +85,8 @@ def tile_picked_zhwy_lin_po_kernel(
         load_w(4)
         load_tab(3)
         nc.sync.dma_start(out=w3_raw[:].bitcast(I32), in_=w3_words[0].bitcast(I32))
-        for a in range(2):
-            nc.sync.dma_start(out=skip_sb[a][:], in_=skip_v[:, :, 2 * CH * a : 2 * CH * (a + 1)])
+        for c in range(NCH):
+            nc.sync.dma_start(out=skip_sb[c][:], in_=skip_v[:, :, CH * c : CH * (c + 1)])
 
         w_bf = [sb(f"w_bf{i}", [P, PACK * (c1 - c0)], BF16) for i, (g, c0, c1) in enumerate(pieces)]
         w_codes = [sb(f"w_codes{g}", [P, H], U32) for g in range(4)]
@@ -202,7 +202,7 @@ def tile_picked_zhwy_lin_po_kernel(
             nc.scalar.activation(carry[c][:], u_ps[c][:], SIGMOID, scale=-1.0)
 
         def difference(c):
-            nc.vector.tensor_tensor(diff[c][:], skip_sb[c // 2][:, :, CH * (c % 2) : CH * (c % 2 + 1)], h_ps[c][:], SUB)
+            nc.vector.tensor_tensor(diff[c][:], skip_sb[c][:], h_ps[c][:], SUB)
 
         def product(eng, c):
             eng.tensor_tensor(prod[c][:], carry[c][:], diff[c][:], MULT)
@@ -222,30 +222,30 @@ def tile_picked_zhwy_lin_po_kernel(
                 out=res_codes[a][:, n0:n1].bitcast(FP8X4), scales=res_sc[:, CH * c0 : CH * c1], in_=res_bf[a][:, PACK * n0 : PACK * n1]
             )
 
-        for c in range(3):
+        for c in range(NCH):
             round_h(c)
+        for c in range(2):
             gate_product(c)
             difference(c)
-        carry_share(0)
-        product(nc.gpsimd, 0)
-        round_h(3)
-        difference(3)
+        gate_product(2)
         gate_product(3)
-        carry_share(1)
-        product(nc.vector, 1)
-        carry_share(2)
-        product(nc.gpsimd, 2)
+        for c in range(NCH):
+            carry_share(c)
+        difference(2)
+        product(nc.vector, 0)
+        product(nc.gpsimd, 1)
+        difference(3)
         total(0)
+        product(nc.vector, 2)
+        product(nc.gpsimd, 3)
         total(1)
-        carry_share(3)
-        product(nc.vector, 3)
-        round_res(nc.scalar.copy, 0, 0, CH)
-        round_res(nc.scalar.copy, 1, 0, CH)
         total(2)
+        for c in range(3):
+            round_res(nc.scalar.copy, c, 0, CH)
+        quant_res(0, 1)
         total(3)
-        round_res(nc.scalar.copy, 2, 0, CH)
         round_res(nc.scalar.copy, 3, 0, CH // 2)
-        quant_res(0, 2)
+        quant_res(1, 2)
         nc.sync.dma_start(out=words_v[:, : 2 * CH], in_=res_codes[0][:].bitcast(I32))
         round_res(nc.vector.tensor_copy, 3, CH // 2, CH)
         quant_res(2, 3)

@@ -165,7 +165,7 @@ def tile_picked_zhwy_lin_po_kernel(
         for i, (a, b) in enumerate(last_spans):
             nc.vector.tensor_copy(last_tiles[i][:], tab_win[3][:].indirect(tok_sb[:, CH // 16 * a : CH // 16 * b]))
         nc.vector.tensor_copy(
-            w3_dealt[:].rearrange("p (t m b) -> p t m b", t=PACK, b=2), w3_raw[:].rearrange("p (m t b) -> p t m b", t=PACK, b=2)
+            w3_dealt[:].bitcast(U16).rearrange("p (t m) -> p t m", t=PACK), w3_raw[:].bitcast(U16).rearrange("p (m t) -> p t m", t=PACK)
         )
         h_passes(3)
 

@@ -65,17 +65,17 @@ def tile_picked_zhwy_lin_po_kernel(
         def load_tab(g):
             nc.sync.dma_start(out=tab_win[g][:].bitcast(I32), in_=tab_src[g].rearrange("p n t -> p (n t)").bitcast(I32))
 
-        def load_planes(eng, dst, src):
+        def load_planes(eng, dst, src, row):
             for q in range(4):
-                eng.dma_start(out=dst[32 * q : 32 * q + 8, :].bitcast(I32), in_=src[:, 4 * q : 4 * q + 4, :].bitcast(I32))
+                eng.dma_start(out=dst[32 * q + row : 32 * q + row + 8, :].bitcast(I32), in_=src[:, 4 * q : 4 * q + 4, :].bitcast(I32))
 
         load_tab(0)
         nc.sync.dma_start(offs_sb[:], offs)
-        load_planes(nc.sync, xs_win, x_scales)
+        load_planes(nc.sync, xs_win, x_scales, 0)
         load_tab(1)
         load_w(0)
         nc.sync.dma_start(tok_sb[:], tok)
-        load_planes(nc.gpsimd, es_win, e_scales)
+        load_planes(nc.gpsimd, es_win, e_scales, 8)
         load_w(1)
         load_tab(2)
         for q in range(4):
@@ -135,7 +135,7 @@ def tile_picked_zhwy_lin_po_kernel(
                         lhsT=w_codes[g][:, mc].bitcast(FP8X4),
                         lhsT_scale=w_sc[g][:, mc],
                         rhs=(picked[g][:, cols] if g < 3 else last_picked[c]).bitcast(FP8X4),
-                        rhs_scale=planes[4 * (g % 2) : P, cols],
+                        rhs_scale=planes[4 * g : P, cols],
                         start=(g == 0 and t == 0),
                         stop=(g == 3 and t == PACK - 1),
                     )

from contextlib import ExitStack

import concourse.mybir as mybir

K, T, S, H = 1024, 1024, 512, 512
FLOPS = 2 * (2 * K * H * S) + 2 * H * H * S

F32 = mybir.dt.float32
BF16 = mybir.dt.bfloat16
I32 = mybir.dt.int32
U32 = mybir.dt.uint32
U16 = mybir.dt.uint16
U8 = mybir.dt.uint8
FP8X4 = mybir.dt.float8_e4m3fn_x4
FP4X4 = mybir.dt.float4_e2m1fn_x4
SIGMOID = mybir.ActivationFunctionType.Sigmoid
SUB = mybir.AluOpType.subtract
MULT = mybir.AluOpType.mult
ADD = mybir.AluOpType.add

P = 128
PACK = 4
KP = P * PACK
CH = 128
NCH = S // CH
V_SHARE = (96, 16, 64, 32, 40)


def tile_picked_zhwy_lin_po_kernel(
    tc, x_words, x_scales, e_words, e_scales, w1, w2, w3_words, w3_scales, skip, offs, tok, out_0, out_1, out_2
):
    nc = tc.nc
    with ExitStack() as ctx:
        keep = ctx.enter_context(tc.tile_pool(name="keep", bufs=1))
        psum = ctx.enter_context(tc.psum_pool(name="psum", bufs=1))

        def sb(name, shape, dtype, tag=None):
            return keep.tile(shape, dtype, name=name, tag=tag or name, align_bytes=64)

        offs_sb = keep.tile([P, S // 16], U16, name="offs_sb")
        tok_sb = keep.tile([P, S // 16], U16, name="tok_sb")

        xs_win = sb("xs_win", [P, T], U8)
        es_win = sb("es_win", [P, T], U8)
        w3s_raw = sb("w3s_raw", [P, H + 4], U8)
        table_out = sb("table_out", [P, 1], F32)
        nc.vector.memset(xs_win[:].bitcast(I32), 0)
        nc.gpsimd.memset(es_win[:].bitcast(I32), 0)
        nc.vector.memset(w3s_raw[:].bitcast(I32), 0)
        nc.scalar.activation(table_out[:], w3s_raw[:, H : H + 4].bitcast(F32), SIGMOID)

        w_src = [w1[0:KP, :], w1[KP:K, :], w2[0:KP, :], w2[KP:K, :]]
        pieces = [(0, 0, H), (1, 0, H), (2, 0, H), (3, 0, H // 2), (3, H // 2, H)]
        w_raw = [sb(f"w_raw{i}", [P, PACK, c1 - c0], F32) for i, (g, c0, c1) in enumerate(pieces)]
        tab_win = [sb(f"tab_win{g}", [P, T], U32) for g in range(4)]
        tab_src = [x_words[0], x_words[1], e_words[0], e_words[1]]
        w3_raw = sb("w3_raw", [P, 2 * H], U8)
        skip_sb = [sb(f"skip{c}", [P, PACK, CH], F32) for c in range(NCH)]
        skip_v = skip.rearrange("(p t) j -> p t j", t=PACK)

        def load_w(i):
            g, c0, c1 = pieces[i]
            nc.sync.dma_start(out=w_raw[i][:], in_=w_src[g].rearrange("(p j) c -> p j c", j=PACK)[:, :, c0:c1])

        def load_tab(g):
            nc.sync.dma_start(out=tab_win[g][:].bitcast(I32), in_=tab_src[g].rearrange("p n t -> p (n t)").bitcast(I32))

        def load_planes(eng, dst, src, row):
            for q in range(4):
                eng.dma_start(out=dst[32 * q + row : 32 * q + row + 8, :].bitcast(I32), in_=src[:, 4 * q : 4 * q + 4, :].bitcast(I32))

        load_tab(0)
        nc.sync.dma_start(offs_sb[:], offs)
        load_planes(nc.sync, xs_win, x_scales, 0)
        load_tab(1)
        load_w(0)
        nc.sync.dma_start(tok_sb[:], tok)
        load_planes(nc.gpsimd, es_win, e_scales, 8)
        load_w(1)
        load_tab(2)
        for q in range(4):
            nc.sync.dma_start(out=w3s_raw[32 * q : 32 * q + 4, :H].bitcast(I32), in_=w3_scales[0, 4 * q : 4 * q + 4, :].bitcast(I32))
        load_w(2)
        load_w(3)
        load_w(4)
        load_tab(3)
        nc.sync.dma_start(out=w3_raw[:].bitcast(I32), in_=w3_words[0].bitcast(I32))
        for c in range(NCH):
            nc.sync.dma_start(out=skip_sb[c][:], in_=skip_v[:, :, CH * c : CH * (c + 1)])

        w_bf = [sb(f"w_bf{i}", [P, PACK * (c1 - c0)], BF16) for i, (g, c0, c1) in enumerate(pieces)]
        w_codes = [sb(f"w_codes{g}", [P, H], U32) for g in range(4)]
        w_sc = [sb(f"w_sc{g}", [P, H], U8) for g in range(4)]
        picked = [sb(f"picked{g}", [P, S], U32) for g in range(3)]
        last_spans = [(0, 1), (1, 2), (2, 4)]
        last_tiles = [sb(f"picked3_{a}", [P, CH * (b - a)], U32) for a, b in last_spans]
        last_picked = [last_tiles[0][:], last_tiles[1][:], last_tiles[2][:, 0:CH], last_tiles[2][:, CH : 2 * CH]]
        xs_picked = sb("xs_picked", [P, S], U8)
        w3_dealt = sb("w3_dealt", [P, 2 * H], U8)
        w3s_dealt = sb("w3s_dealt", [P, H], U8)

        def round_w(i):
            dst = w_bf[i][:].rearrange("p (t m j) -> p m j t", t=PACK, j=PACK)
            src = w_raw[i][:].rearrange("p j (m t) -> p m j t", t=PACK)
            if V_SHARE[i]:
                nc.vector.tensor_copy(dst[:, : V_SHARE[i]], src[:, : V_SHARE[i]])
            nc.scalar.copy(dst[:, V_SHARE[i] :], src[:, V_SHARE[i] :])

        def quant_w(i):
            g, c0, c1 = pieces[i]
            width = c1 - c0
            if width == H:
                nc.vector.quantize_mx(out=w_codes[g][:].bitcast(FP8X4), scales=w_sc[g][:], in_=w_bf[i][:])
                return
            for t in range(PACK):
                cols = slice(P * t + c0 // PACK, P * t + c1 // PACK)
                nc.vector.quantize_mx(
                    out=w_codes[g][:, cols].bitcast(FP8X4), scales=w_sc[g][:, cols], in_=w_bf[i][:, width * t : width * (t + 1)]
                )

        def gather(g):
            nc.vector.tensor_copy(picked[g][:], tab_win[g][:].indirect((offs_sb if g < 2 else tok_sb)[:]))

        h_ps = [psum.tile([P, PACK, CH], F32, name=f"h_ps{c}", tag=f"h_ps{c}") for c in range(NCH)]
        u_ps = [psum.tile([P, PACK, CH], F32, name=f"u_ps{c}", tag=f"u_ps{c}") for c in range(NCH)]

        def h_passes(g):
            planes = xs_picked if g < 2 else es_picked
            for c in range(NCH):
                cols = slice(CH * c, CH * (c + 1))
                for t in range(PACK):
                    mc = slice(P * t, P * (t + 1))
                    nc.tensor.matmul_mx(
                        out=h_ps[c][:, t, :],
                        lhsT=w_codes[g][:, mc].bitcast(FP8X4),
                        lhsT_scale=w_sc[g][:, mc],
                        rhs=(picked[g][:, cols] if g < 3 else last_picked[c]).bitcast(FP8X4),
                        rhs_scale=planes[4 * g : P, cols],
                        start=(g == 0 and t == 0),
                        stop=(g == 3 and t == PACK - 1),
                    )

        gather(0)
        nc.vector.tensor_copy(xs_picked[:], xs_win[:].indirect(offs_sb[:]))
        gather(1)
        round_w(0)
        quant_w(0)
        h_passes(0)
        round_w(1)
        es_picked = sb("es_picked", [P, S], U8, tag="w_bf0")
        nc.vector.tensor_copy(es_picked[:], es_win[:].indirect(tok_sb[:]))
        quant_w(1)
        h_passes(1)
        gather(2)
        nc.vector.tensor_copy(
            w3s_dealt[:].rearrange("p (t m) -> p t m", t=PACK), w3s_raw[:, :H].rearrange("p (m t) -> p t m", t=PACK)
        )
        round_w(2)
        quant_w(2)
        h_passes(2)
        round_w(3)
        quant_w(3)
        round_w(4)
        quant_w(4)
        for i, (a, b) in enumerate(last_spans):
            nc.vector.tensor_copy(last_tiles[i][:], tab_win[3][:].indirect(tok_sb[:, CH // 16 * a : CH // 16 * b]))
        nc.vector.tensor_copy(
            w3_dealt[:].bitcast(U16).rearrange("p (t m) -> p t m", t=PACK), w3_raw[:].bitcast(U16).rearrange("p (m t) -> p t m", t=PACK)
        )
        h_passes(3)

        h_bf = [sb(f"h_bf{c}", [P, CH * PACK], BF16) for c in range(NCH)]
        h_codes = [sb(f"h_codes{c}", [P, CH], U32) for c in range(NCH)]
        h_sc = [sb(f"h_sc{c}", [P, CH], U8) for c in range(NCH)]
        carry = [sb(f"carry{c}", [P, PACK, CH], F32) for c in range(NCH)]
        diff = [sb(f"diff{c}", [P, PACK, CH], F32) for c in range(NCH)]
        prod = [sb(f"prod{c}", [P, PACK, CH], F32) for c in range(NCH)]
        res = [sb(f"res{c}", [P, PACK, CH], F32) for c in range(NCH)]
        res_bf = [sb(f"res_bf{a}", [P, 2 * CH * PACK], BF16) for a in range(2)]
        res_codes = [sb(f"res_codes{a}", [P, 2 * CH], U32) for a in range(2)]
        res_sc = sb("res_sc", [P, S], U8)
        out_v = out_0.rearrange("(p t) j -> p t j", t=PACK)
        words_v = out_1[0].rearrange("p n t -> p (n t)").bitcast(I32)

        def round_h(c):
            nc.scalar.copy(h_bf[c][:].rearrange("p (n t) -> p n t", t=PACK), h_ps[c][:].rearrange("p t n -> p n t"))

        def gate_product(c):
            nc.vector.quantize_mx(out=h_codes[c][:].bitcast(FP8X4), scales=h_sc[c][:], in_=h_bf[c][:])
            for t in range(PACK):
                nc.tensor.matmul_mx(
                    out=u_ps[c][:, t, :],
                    lhsT=w3_dealt[:, 2 * P * t : 2 * P * (t + 1)].bitcast(FP4X4),
                    lhsT_scale=w3s_dealt[:, P * t : P * (t + 1)],
                    rhs=h_codes[c][:].bitcast(FP8X4),
                    rhs_scale=h_sc[c][:],
                    start=True,
                    stop=True,
                )

        def carry_share(c):
            nc.scalar.activation(carry[c][:], u_ps[c][:], SIGMOID, scale=-1.0)

        def difference(c):
            nc.vector.tensor_tensor(diff[c][:], skip_sb[c][:], h_ps[c][:], SUB)

        def product(eng, c):
            eng.tensor_tensor(prod[c][:], carry[c][:], diff[c][:], MULT)

        def total(c):
            nc.vector.tensor_tensor(res[c][:], h_ps[c][:], prod[c][:], ADD)
            nc.sync.dma_start(out=out_v[:, :, CH * c : CH * (c + 1)], in_=res[c][:])

        def round_res(copy, c, n0, n1):
            base = CH * (c % 2)
            dst = res_bf[c // 2][:, PACK * (base + n0) : PACK * (base + n1)].rearrange("p (n i t) -> p n t i", i=4, t=PACK)
            copy(dst, res[c][:, :, n0:n1].rearrange("p t (n i) -> p n t i", i=4))

        def quant_res(c0, c1):
            a, n0, n1 = c0 // 2, CH * (c0 % 2), CH * (c0 % 2 + c1 - c0)
            nc.vector.quantize_mx(
                out=res_codes[a][:, n0:n1].bitcast(FP8X4), scales=res_sc[:, CH * c0 : CH * c1], in_=res_bf[a][:, PACK * n0 : PACK * n1]
            )

        for c in range(NCH):
            round_h(c)
        for c in range(2):
            gate_product(c)
            difference(c)
        gate_product(2)
        gate_product(3)
        for c in range(NCH):
            carry_share(c)
        difference(2)
        product(nc.vector, 0)
        product(nc.gpsimd, 1)
        difference(3)
        total(0)
        product(nc.vector, 2)
        product(nc.gpsimd, 3)
        total(1)
        total(2)
        for c in range(3):
            round_res(nc.scalar.copy, c, 0, CH)
        quant_res(0, 1)
        total(3)
        round_res(nc.scalar.copy, 3, 0, CH // 2)
        quant_res(1, 2)
        nc.sync.dma_start(out=words_v[:, : 2 * CH], in_=res_codes[0][:].bitcast(I32))
        round_res(nc.vector.tensor_copy, 3, CH // 2, CH)
        quant_res(2, 3)
        quant_res(3, 4)
        nc.sync.dma_start(out=words_v[:, 2 * CH :], in_=res_codes[1][:].bitcast(I32))
        for q in range(4):
            eng = nc.sync if q % 2 == 0 else nc.scalar
            eng.dma_start(out=out_2[0, 4 * q : 4 * q + 4, :].bitcast(I32), in_=res_sc[32 * q : 32 * q + 4, :].bitcast(I32))
